import numpy as np
import ml_dtypes


def mxq(x, axis, fmt="e4m3"):
    dtype, down = {"e4m3": (ml_dtypes.float8_e4m3fn, 7), "e5m2": (ml_dtypes.float8_e5m2, 14)}[fmt]
    v = np.moveaxis(np.asarray(x, np.float32).astype(ml_dtypes.bfloat16).astype(np.float64), axis, -1)
    blocks = v.reshape(v.shape[:-1] + (-1, 32))
    amax = np.abs(blocks).max(-1, keepdims=True)
    byte = np.maximum(np.where(amax > 0, np.frexp(amax)[1] - 1 + 127, 0) - down, 1)
    scale = np.exp2(byte - 127.0)
    codes = (blocks / scale).astype(np.float32).astype(dtype).astype(np.float64)
    return np.moveaxis((codes * scale).reshape(v.shape), -1, axis)


WIDE = False


def mx_kscale(k):
    if not WIDE:
        return np.ones(k)
    levels = np.array([10, -10, 5, -5, 0])
    if k % 512:
        return np.exp2(np.random.permutation(np.resize(levels, k // 32))).repeat(32)
    a = np.empty((k // 512, 16))
    for p in range(k // 512):
        a[p, :8] = np.random.permutation(np.resize(levels, 8))
        for g in range(8):
            far = levels[np.abs(levels - a[p, g]) >= 10]
            a[p, g + 8] = far[np.random.randint(len(far))]
    return np.exp2(a.ravel()).repeat(32)


def f64(x):
    return np.asarray(x).astype(np.float64)


def striped(idx):
    return np.tile(idx.reshape(-1, 16).T, (8, 1)).astype(np.uint16)


def unstriped(offs):
    return offs[:16].T.reshape(-1).astype(np.int64)


def pack_weight(w):
    k, n = w.shape
    w = f64(np.asarray(w, np.float32).astype(ml_dtypes.bfloat16)).reshape(k // 32, 32, n)
    amax = np.abs(w).max(1)
    byte = np.clip(np.where(amax > 0, np.frexp(amax)[1] - 1 + 127 - 7, 1), 1, 254)
    scaled = (w * np.exp2(127.0 - byte)[:, None, :]).reshape(k, n).astype(np.float32)
    words = np.ascontiguousarray(scaled.reshape(k // 512, 128, 4, n).transpose(0, 1, 3, 2)).astype(ml_dtypes.float8_e4m3fn).view(np.uint8)
    return words, np.ascontiguousarray(byte.astype(np.uint8).reshape(k // 512, 16, n))


def unpack_weight(words, scales):
    g, p, n, _ = words.shape
    vals = np.ascontiguousarray(words).view(ml_dtypes.float8_e4m3fn).astype(np.float64) * np.repeat(np.exp2(scales.astype(np.float64) - 127.0), 8, axis=1)[..., None]
    return vals.transpose(0, 1, 3, 2).reshape(g * 512, n)


def relu(v):
    return np.maximum(v, 0.0)


K, T, S, H, N, D = 512, 2048, 512, 512, 256, 2
P = 2 ** 7


def setup_inputs():
    n = np.random.standard_normal
    s = mx_kscale(K)[:, None]
    u = mx_kscale(H)
    packed_xT = pack_weight(n((K, T)) * s)
    return {
        "x_words": packed_xT[0],
        "x_scales": packed_xT[1],
        "w1": (n((K, H)) / np.sqrt(K) / s * u).astype(np.float32),
        "w2": (n((H, N)) / np.sqrt(H) / u[:, None]).astype(np.float32),
        "kern": (np.tile(0.7 * n((D, 1, S)), (1, P, 1))).astype(np.float32),
        "cur": (n((N, S))).astype(np.float32),
        "fire": (np.tile((np.random.uniform(size=S) < 0.5) * 1.0, (P, 1))).astype(np.float32),
        "offs": striped(np.random.permutation(T)[:S]),
        "pos1": striped(np.random.permutation(S)[:S]),
        "pos2": striped(np.random.permutation(S)[:S]),
    }


def reference(x_words, x_scales, w1, w2, kern, cur, fire, offs, pos1, pos2):
    xq = unpack_weight(x_words, x_scales)[:, unstriped(offs)]
    y = mxq(f64(w1), 0, "e4m3").T @ xq
    h = relu(y + y[:, unstriped(pos1)] * f64(kern)[0, :1] + y[:, unstriped(pos2)] * f64(kern)[1, :1])
    rr = mxq(f64(w2), 0, "e4m3").T @ mxq(h, 0, "e4m3")
    return np.tanh(f64(cur) + rr * f64(fire)[:1])

@@ -1,0 +1,233 @@
+from contextlib import ExitStack
+
+import concourse.mybir as mybir
+from concourse.masks import make_identity
+
+K, T, S, H, N = 512, 2048, 512, 512, 256
+FLOPS = 2 * K * H * S + 2 * H * N * S
+
+F32 = mybir.dt.float32
+BF16 = mybir.dt.bfloat16
+I32 = mybir.dt.int32
+U32 = mybir.dt.uint32
+U16 = mybir.dt.uint16
+U8 = mybir.dt.uint8
+FP8X4 = mybir.dt.float8_e4m3fn_x4
+ALU = mybir.AluOpType
+ACT = mybir.ActivationFunctionType
+
+P = 128
+PACK = 4
+PER_COL = 16
+TILES = H // P
+BLOCKS = S // P
+HALVES = N // P
+CHUNKS = ((0, 2), (2, 3), (3, 4))
+
+
+def interleave(nc, grouped, raw):
+    nc.scalar.copy(
+        out=grouped.rearrange("p (c i t) -> p c t i", i=4, t=PACK),
+        in_=raw.rearrange("p t (c i) -> p c t i", i=4),
+    )
+
+
+def tile_picked_ynca_tanh_p_kernel(tc, x_words, x_scales, w1, w2, kern, cur, fire, offs, pos1, pos2, out):
+    nc = tc.nc
+    with ExitStack() as ctx:
+        keep = ctx.enter_context(tc.tile_pool(name="keep", bufs=1))
+        sums = ctx.enter_context(tc.psum_pool(name="sums", bufs=1))
+        ring = ctx.enter_context(tc.psum_pool(name="ring", bufs=4))
+
+        def sb(shape, dtype, name, tag=None):
+            return keep.tile(shape, dtype, name=name, tag=tag or name, align_bytes=64)
+
+        def bank(shape, name):
+            return ring.tile(shape, F32, name=name, tag="bank")
+
+        scale_table = sb([P, T], U8, "scale_table")
+        nc.vector.memset(scale_table[:].bitcast(I32), 0)
+        warm = sb([P, 1], F32, "warm")
+        warm_out = sb([P, 1], F32, "warm_out")
+        nc.vector.memset(warm[:], 0.0)
+
+        offs_sb = keep.tile([P, S // PER_COL], U16, name="offs_sb")
+        nc.sync.dma_start(offs_sb[:], offs)
+        nc.scalar.activation(warm_out[:], warm[:], ACT.Tanh)
+
+        w1_rows = w1.rearrange("(p t) c -> p t c", t=PACK)
+        w1_raw = [sb([P, PACK, P], F32, "w1_raw%d" % t) for t in range(2)]
+        w1_rest = sb([P, PACK, 2 * P], F32, "w1_rest")
+        word_table = sb([P, T], U32, "word_table")
+        kern_sb = [sb([P, S], F32, "kern%d" % n) for n in range(2)]
+        pos_sb = [keep.tile([P, S // PER_COL], U16, name="pos%d" % n) for n in range(2)]
+        w2_raw = sb([P, PACK, N], F32, "w2_raw")
+        fire_rows = sb([P, P], F32, "fire_rows")
+        cur_sb = sb([P, HALVES, S], F32, "cur_sb")
+
+        nc.sync.dma_start(w1_raw[0][:], w1_rows[:, :, 0:P])
+        for q in range(4):
+            nc.sync.dma_start(
+                scale_table[32 * q : 32 * q + 4, :].bitcast(I32), x_scales[0, 4 * q : 4 * q + 4, :].bitcast(I32)
+            )
+        nc.sync.dma_start(word_table[:].bitcast(I32), x_words[0].rearrange("p n t -> p (n t)").bitcast(I32))
+        nc.sync.dma_start(w1_raw[1][:], w1_rows[:, :, P : 2 * P])
+        nc.sync.dma_start(pos_sb[0][:], pos1)
+        nc.sync.dma_start(kern_sb[0][:], kern[0])
+        nc.sync.dma_start(pos_sb[1][:], pos2)
+        nc.sync.dma_start(kern_sb[1][:], kern[1])
+        nc.sync.dma_start(w1_rest[:], w1_rows[:, :, 2 * P :])
+        nc.sync.dma_start(fire_rows[:], fire[0 : P // BLOCKS, :].rearrange("r (b j) -> (r b) j", j=P))
+        nc.sync.dma_start(w2_raw[:], w2.rearrange("(p t) c -> p t c", t=PACK))
+        nc.sync.dma_start(cur_sb[:], cur.rearrange("(h p) j -> p h j", p=P))
+
+        ident = sb([P, P], F32, "ident")
+        make_identity(nc, ident[:])
+
+        x_scale = sb([P, S], U8, "x_scale")
+        nc.vector.tensor_copy(x_scale[:], scale_table[:].indirect(offs_sb[:]))
+
+        w1_views = [w1_raw[0][:], w1_raw[1][:], w1_rest[:, :, 0:P], w1_rest[:, :, P:]]
+        w1_codes = [sb([P, P], U32, "w1_codes%d" % t) for t in range(TILES)]
+        w1_scale = [sb([P, P], U8, "w1_scale%d" % t) for t in range(TILES)]
+
+        def quantise_w1(t):
+            grouped = sb([P, P * PACK], BF16, "w1_grouped%d" % t, tag="stage%d" % t)
+            interleave(nc, grouped[:], w1_views[t])
+            nc.vector.quantize_mx(out=w1_codes[t][:].bitcast(FP8X4), scales=w1_scale[t][:], in_=grouped[:])
+
+        x_codes = sb([P, S], U32, "x_codes")
+        y = [sb([P, S], F32, "y%d" % t) for t in range(TILES)]
+
+        def first_product(t, cols, name):
+            acc = bank([P, cols.stop - cols.start], name)
+            nc.tensor.matmul_mx(
+                out=acc[:],
+                lhsT=w1_codes[t][:].bitcast(FP8X4),
+                lhsT_scale=w1_scale[t][:],
+                rhs=x_codes[:, cols].bitcast(FP8X4),
+                rhs_scale=x_scale[:, cols],
+                start=True,
+                stop=True,
+            )
+            return acc
+
+        quantise_w1(0)
+        half = S // 2
+        for a in range(2):
+            cols = slice(a * half, (a + 1) * half)
+            nc.vector.tensor_copy(
+                x_codes[:, cols], word_table[:].indirect(offs_sb[:, cols.start // PER_COL : cols.stop // PER_COL])
+            )
+        acc = first_product(0, slice(0, half), "y0_low")
+        nc.scalar.copy(y[0][:, 0:half], acc[:])
+        acc = first_product(0, slice(half, S), "y0_high")
+        nc.vector.tensor_copy(y[0][:, half:], acc[:])
+
+        def make_y(t):
+            quantise_w1(t)
+            acc = first_product(t, slice(0, S), "y_acc%d" % t)
+            nc.scalar.copy(y[t][:], acc[:])
+
+        pre = [sums.tile([P, H], F32, name="pre%d" % b) for b in range(BLOCKS)]
+        fire_col = sb([P, BLOCKS], F32, "fire_col")
+        w2_codes = sb([P, N], U32, "w2_codes")
+        w2_scale = sb([P, N], U8, "w2_scale")
+
+        def perceive(t, first, last, seen):
+            cols = slice(first * P, last * P)
+            for n in range(2):
+                nc.vector.tensor_tensor(
+                    seen[n],
+                    y[t][:].indirect(pos_sb[n][:, cols.start // PER_COL : cols.stop // PER_COL]),
+                    kern_sb[n][:, cols],
+                    ALU.mult,
+                )
+            terms = (y[t][:, cols], seen[0], seen[1])
+            for place, term in enumerate(terms):
+                for b in range(first, last):
+                    nc.tensor.matmul(
+                        pre[b][:, t * P : (t + 1) * P],
+                        term[:, (b - first) * P : (b - first + 1) * P],
+                        ident[:],
+                        start=(place == 0),
+                        stop=(place == len(terms) - 1),
+                        is_transpose=True,
+                    )
+
+        def prepare_second():
+            turned = bank([P, P], "fire_turned")
+            nc.tensor.transpose(turned[:], fire_rows[:], ident[:])
+            nc.scalar.copy(fire_col[:], turned[:, 0:BLOCKS])
+            grouped = sb([P, N * PACK], BF16, "w2_grouped", tag="stage%d" % TILES)
+            interleave(nc, grouped[:], w2_raw[:])
+            nc.vector.quantize_mx(out=w2_codes[:].bitcast(FP8X4), scales=w2_scale[:], in_=grouped[:])
+
+        h_grouped = [sb([P, P * PACK], BF16, "h_grouped%d" % b) for b in range(BLOCKS)]
+
+        def turn_back(b):
+            h_rows = sb([P, H], BF16, "h_rows%d" % b, tag="rows%d" % b)
+            nc.scalar.activation(
+                h_rows[:].rearrange("j (u p e) -> j u p e", u=2, e=2),
+                pre[b][:].rearrange("j (p u e) -> j u p e", u=2, e=2),
+                ACT.Relu,
+                scale=fire_col[:, b : b + 1],
+            )
+            pairs = h_rows[:].bitcast(F32)
+            turned = bank([P, 2, P], "h_turned%d" % b)
+            for u in range(2):
+                nc.tensor.transpose(turned[:, u, :], pairs[:, u * P : (u + 1) * P], ident[:])
+            nc.scalar.copy(
+                h_grouped[b][:].bitcast(F32).rearrange("p (j u) -> p j u", u=2),
+                turned[:].rearrange("p u j -> p j u"),
+            )
+
+        out_rows = out.rearrange("(h p) j -> p h j", p=P)
+
+        def finish(b):
+            cols = slice(b * P, (b + 1) * P)
+            h_codes = sb([P, P], U32, "h_codes%d" % b)
+            h_scale = sb([P, P], U8, "h_scale%d" % b)
+            nc.vector.quantize_mx(out=h_codes[:].bitcast(FP8X4), scales=h_scale[:], in_=h_grouped[b][:])
+            rr = bank([P, HALVES, P], "rr%d" % b)
+            for h in range(HALVES):
+                nc.tensor.matmul_mx(
+                    out=rr[:, h, :],
+                    lhsT=w2_codes[:, h * P : (h + 1) * P].bitcast(FP8X4),
+                    lhsT_scale=w2_scale[:, h * P : (h + 1) * P],
+                    rhs=h_codes[:].bitcast(FP8X4),
+                    rhs_scale=h_scale[:],
+                    start=True,
+                    stop=True,
+                )
+            moved = sb([P, HALVES, P], F32, "moved%d" % b)
+            nc.vector.tensor_tensor(moved[:], rr[:], cur_sb[:, :, cols], ALU.add)
+            state = sb([P, HALVES, P], F32, "state%d" % b)
+            nc.scalar.activation(state[:], moved[:], ACT.Tanh)
+            nc.sync.dma_start(out_rows[:, :, cols], state[:])
+
+        first, last = CHUNKS[0]
+        width = (last - first) * P
+        for t in range(TILES):
+            if t + 1 < TILES:
+                make_y(t + 1)
+            else:
+                prepare_second()
+            one = sb([P, width], F32, "seen%d_0" % t, tag="stage%d" % (t + 1))
+            two = sb([P, width], F32, "seen%d_1" % t, tag="other%d" % t)
+            perceive(t, first, last, (one[:], two[:]))
+        done = list(range(first, last))
+        for c, tag in ((1, "other2"), (2, "rows0")):
+            for b in done:
+                turn_back(b)
+            first, last = CHUNKS[c]
+            seen = sb([P, 2 * TILES * P], F32, "seen_late%d" % c, tag=tag)
+            if c == 2:
+                for b in range(*CHUNKS[0]):
+                    finish(b)
+            for t in range(TILES):
+                perceive(t, first, last, [seen[:, (2 * t + n) * P : (2 * t + n + 1) * P] for n in range(2)])
+            done = list(range(first, last))
+        finish(2)
+        turn_back(3)
+        finish(3)

@@ -22,7 +22,9 @@ PER_COL = 16
 TILES = H // P
 BLOCKS = S // P
 HALVES = N // P
-CHUNKS = ((0, 2), (2, 3), (3, 4))
+GROUPS = ((0, 2), (2, 3), (3, 4))
+SPARE = 16
+EARLY = 2
 
 
 def interleave(nc, grouped, raw):
@@ -36,14 +38,15 @@ def tile_picked_ynca_tanh_p_kernel(tc, x_words, x_scales, w1, w2, kern, cur, fir
     nc = tc.nc
     with ExitStack() as ctx:
         keep = ctx.enter_context(tc.tile_pool(name="keep", bufs=1))
-        sums = ctx.enter_context(tc.psum_pool(name="sums", bufs=1))
-        ring = ctx.enter_context(tc.psum_pool(name="ring", bufs=4))
+        ring = ctx.enter_context(tc.psum_pool(name="ring", bufs=7))
+        shared = ctx.enter_context(tc.psum_pool(name="shared", bufs=1))
 
         def sb(shape, dtype, name, tag=None):
             return keep.tile(shape, dtype, name=name, tag=tag or name, align_bytes=64)
 
         def bank(shape, name):
-            return ring.tile(shape, F32, name=name, tag="bank")
+            pool = shared if name in ("y_acc3", "fire_turned", "h_turned0", "pre_high3", "rr2_0") else ring
+            return pool.tile(shape, F32, name=name, tag="bank")
 
         scale_table = sb([P, T], U8, "scale_table")
         nc.vector.memset(scale_table[:].bitcast(I32), 0)
@@ -61,7 +64,7 @@ def tile_picked_ynca_tanh_p_kernel(tc, x_words, x_scales, w1, w2, kern, cur, fir
         word_table = sb([P, T], U32, "word_table")
         kern_sb = [sb([P, S], F32, "kern%d" % n) for n in range(2)]
         pos_sb = [keep.tile([P, S // PER_COL], U16, name="pos%d" % n) for n in range(2)]
-        w2_raw = sb([P, PACK, N], F32, "w2_raw")
+        w2_raw = sb([P, PACK, N], F32, "w2_raw", tag="y3")
         fire_rows = sb([P, P], F32, "fire_rows")
         cur_sb = sb([P, HALVES, S], F32, "cur_sb")
 
@@ -88,7 +91,7 @@ def tile_picked_ynca_tanh_p_kernel(tc, x_words, x_scales, w1, w2, kern, cur, fir
         nc.vector.tensor_copy(x_scale[:], scale_table[:].indirect(offs_sb[:]))
 
         w1_views = [w1_raw[0][:], w1_raw[1][:], w1_rest[:, :, 0:P], w1_rest[:, :, P:]]
-        w1_codes = [sb([P, P], U32, "w1_codes%d" % t) for t in range(TILES)]
+        w1_codes = [sb([P, P], U32, "w1_codes%d" % t, tag="codes%d" % t) for t in range(TILES)]
         w1_scale = [sb([P, P], U8, "w1_scale%d" % t) for t in range(TILES)]
 
         def quantise_w1(t):
@@ -97,7 +100,9 @@ def tile_picked_ynca_tanh_p_kernel(tc, x_words, x_scales, w1, w2, kern, cur, fir
             nc.vector.quantize_mx(out=w1_codes[t][:].bitcast(FP8X4), scales=w1_scale[t][:], in_=grouped[:])
 
         x_codes = sb([P, S], U32, "x_codes")
-        y = [sb([P, S], F32, "y%d" % t) for t in range(TILES)]
+        y = [sb([P, S + SPARE if t < EARLY else S], F32, "y%d" % t) for t in range(TILES - 1)]
+        for t in range(EARLY):
+            nc.gpsimd.memset(y[t][:, S:], 0.0)
 
         def first_product(t, cols, name):
             acc = bank([P, cols.stop - cols.start], name)
@@ -122,77 +127,82 @@ def tile_picked_ynca_tanh_p_kernel(tc, x_words, x_scales, w1, w2, kern, cur, fir
         acc = first_product(0, slice(0, half), "y0_low")
         nc.scalar.copy(y[0][:, 0:half], acc[:])
         acc = first_product(0, slice(half, S), "y0_high")
-        nc.vector.tensor_copy(y[0][:, half:], acc[:])
+        nc.scalar.copy(y[0][:, half:S], acc[:])
 
         def make_y(t):
             quantise_w1(t)
             acc = first_product(t, slice(0, S), "y_acc%d" % t)
-            nc.scalar.copy(y[t][:], acc[:])
+            if t == TILES - 1:
+                interleave(nc, w2_grouped[:], w2_raw[:])
+                y.append(sb([P, S], F32, "y%d" % t))
+            nc.scalar.copy(y[t][:, 0:S], acc[:])
 
-        pre = [sums.tile([P, H], F32, name="pre%d" % b) for b in range(BLOCKS)]
         fire_col = sb([P, BLOCKS], F32, "fire_col")
         w2_codes = sb([P, N], U32, "w2_codes")
         w2_scale = sb([P, N], U8, "w2_scale")
 
-        def perceive(t, first, last, seen):
+        def look_up(t, n, first, last, tag, seen=None):
             cols = slice(first * P, last * P)
-            for n in range(2):
-                nc.vector.tensor_tensor(
-                    seen[n],
-                    y[t][:].indirect(pos_sb[n][:, cols.start // PER_COL : cols.stop // PER_COL]),
-                    kern_sb[n][:, cols],
-                    ALU.mult,
-                )
-            terms = (y[t][:, cols], seen[0], seen[1])
-            for place, term in enumerate(terms):
-                for b in range(first, last):
-                    nc.tensor.matmul(
-                        pre[b][:, t * P : (t + 1) * P],
-                        term[:, (b - first) * P : (b - first + 1) * P],
-                        ident[:],
-                        start=(place == 0),
-                        stop=(place == len(terms) - 1),
-                        is_transpose=True,
-                    )
+            if seen is None:
+                seen = sb([P, cols.stop - cols.start], F32, "seen%d_%d_%d" % (t, n, first), tag=tag)[:]
+            nc.vector.tensor_tensor(
+                seen,
+                y[t][:].indirect(pos_sb[n][:, cols.start // PER_COL : cols.stop // PER_COL]),
+                kern_sb[n][:, cols],
+                ALU.mult,
+            )
+            return seen
+
+        def add_turned(target, term, start=False, stop=False):
+            nc.tensor.matmul(target, term, ident[:], start=start, stop=stop, is_transpose=True)
+
+        def block(b, first=0):
+            return slice((b - first) * P, (b - first + 1) * P)
+
+        w2_grouped = sb([P, N * PACK], BF16, "w2_grouped")
 
         def prepare_second():
             turned = bank([P, P], "fire_turned")
             nc.tensor.transpose(turned[:], fire_rows[:], ident[:])
             nc.scalar.copy(fire_col[:], turned[:, 0:BLOCKS])
-            grouped = sb([P, N * PACK], BF16, "w2_grouped", tag="stage%d" % TILES)
-            interleave(nc, grouped[:], w2_raw[:])
-            nc.vector.quantize_mx(out=w2_codes[:].bitcast(FP8X4), scales=w2_scale[:], in_=grouped[:])
 
-        h_grouped = [sb([P, P * PACK], BF16, "h_grouped%d" % b) for b in range(BLOCKS)]
+        h_rows = [sb([P, H], BF16, "h_rows%d" % b) for b in range(BLOCKS)]
 
-        def turn_back(b):
-            h_rows = sb([P, H], BF16, "h_rows%d" % b, tag="rows%d" % b)
+        def rectify(b, part, pre):
+            rows = h_rows[b][:].rearrange("j (u p e) -> j u p e", u=2, e=2)
             nc.scalar.activation(
-                h_rows[:].rearrange("j (u p e) -> j u p e", u=2, e=2),
-                pre[b][:].rearrange("j (p u e) -> j u p e", u=2, e=2),
+                rows[:, :, part * (P // 2) : (part + 1) * (P // 2), :],
+                pre.rearrange("j (p u e) -> j u p e", u=2, e=2),
                 ACT.Relu,
                 scale=fire_col[:, b : b + 1],
             )
-            pairs = h_rows[:].bitcast(F32)
-            turned = bank([P, 2, P], "h_turned%d" % b)
-            for u in range(2):
-                nc.tensor.transpose(turned[:, u, :], pairs[:, u * P : (u + 1) * P], ident[:])
-            nc.scalar.copy(
-                h_grouped[b][:].bitcast(F32).rearrange("p (j u) -> p j u", u=2),
-                turned[:].rearrange("p u j -> p j u"),
-            )
+
+        def turn_back(first, last):
+            grouped = sb([P, (last - first) * P * PACK], BF16, "h_grouped%d" % first)
+            words = grouped[:].bitcast(F32)
+            for b in range(first, last):
+                turned = bank([P, 2, P], "h_turned%d" % b)
+                pairs = h_rows[b][:].bitcast(F32)
+                for u in range(2):
+                    nc.tensor.transpose(turned[:, u, :], pairs[:, block(u)], ident[:])
+                nc.scalar.copy(
+                    words[:, 2 * P * (b - first) : 2 * P * (b - first + 1)].rearrange("p (j u) -> p j u", u=2),
+                    turned[:].rearrange("p u j -> p j u"),
+                )
+            return grouped
 
         out_rows = out.rearrange("(h p) j -> p h j", p=P)
 
-        def finish(b):
-            cols = slice(b * P, (b + 1) * P)
-            h_codes = sb([P, P], U32, "h_codes%d" % b)
-            h_scale = sb([P, P], U8, "h_scale%d" % b)
-            nc.vector.quantize_mx(out=h_codes[:].bitcast(FP8X4), scales=h_scale[:], in_=h_grouped[b][:])
-            rr = bank([P, HALVES, P], "rr%d" % b)
+        def second_product(first, last, grouped, parts):
+            width = (last - first) * P
+            h_codes = sb([P, width], U32, "h_codes%d" % first)
+            h_scale = sb([P, width], U8, "h_scale%d" % first)
+            nc.vector.quantize_mx(out=h_codes[:].bitcast(FP8X4), scales=h_scale[:], in_=grouped[:])
+            per = HALVES // parts
+            rr = [bank([P, per, width], "rr%d_%d" % (first, i)) for i in range(parts)]
             for h in range(HALVES):
                 nc.tensor.matmul_mx(
-                    out=rr[:, h, :],
+                    out=rr[h // per][:, h % per, :],
                     lhsT=w2_codes[:, h * P : (h + 1) * P].bitcast(FP8X4),
                     lhsT_scale=w2_scale[:, h * P : (h + 1) * P],
                     rhs=h_codes[:].bitcast(FP8X4),
@@ -200,34 +210,68 @@ def tile_picked_ynca_tanh_p_kernel(tc, x_words, x_scales, w1, w2, kern, cur, fir
                     start=True,
                     stop=True,
                 )
-            moved = sb([P, HALVES, P], F32, "moved%d" % b)
-            nc.vector.tensor_tensor(moved[:], rr[:], cur_sb[:, :, cols], ALU.add)
-            state = sb([P, HALVES, P], F32, "state%d" % b)
-            nc.scalar.activation(state[:], moved[:], ACT.Tanh)
-            nc.sync.dma_start(out_rows[:, :, cols], state[:])
+            return rr
 
-        first, last = CHUNKS[0]
-        width = (last - first) * P
-        for t in range(TILES):
-            if t + 1 < TILES:
-                make_y(t + 1)
+        def update(first, last, rr):
+            cols = slice(first * P, last * P)
+            per = HALVES // len(rr)
+            for i, part in enumerate(rr):
+                rows = slice(i * per, (i + 1) * per)
+                moved = sb([P, per, cols.stop - cols.start], F32, "moved%d_%d" % (first, i))
+                nc.vector.tensor_tensor(moved[:], part[:], cur_sb[:, rows, cols], ALU.add)
+                state = sb([P, per, cols.stop - cols.start], F32, "state%d_%d" % (first, i), tag="fire_col" if first == 0 else None)
+                nc.scalar.activation(state[:], moved[:], ACT.Tanh)
+                nc.sync.dma_start(out_rows[:, rows, cols], state[:])
+
+        low = [bank([P, 2, EARLY * P], "pre_low%d" % i) for i in range(BLOCKS // 2)]
+        make_y(1)
+        tags = (("stage1", "free0"), ("stage2", "stage3"))
+        for t in range(EARLY):
+            if t == 1:
+                make_y(2)
+                make_y(3)
+            for b in range(BLOCKS):
+                add_turned(low[b // 2][:, b % 2, block(t)], y[t][:, block(b)], start=(t == 0 and b % 2 == 0))
+            for n in range(2):
+                seen = look_up(t, n, 0, BLOCKS, tags[t][n])
+                for b in range(BLOCKS):
+                    closing = t == EARLY - 1 and n == 1 and b % 2 == 1
+                    add_turned(low[b // 2][:, b % 2, block(t)], seen[:, block(b)], stop=closing)
+        prepare_second()
+        for b in range(BLOCKS):
+            rectify(b, 0, low[b // 2][:, b % 2, :])
+        grouped = []
+        for first, last in GROUPS:
+            if first == GROUPS[-1][0]:
+                nc.vector.quantize_mx(out=w2_codes[:].bitcast(FP8X4), scales=w2_scale[:], in_=w2_grouped[:])
+                rr_first = second_product(*GROUPS[0], grouped[0], 1)
+            high = [bank([P, (TILES - EARLY) * P], "pre_high%d" % b) for b in range(first, last)]
+            cols = slice(first * P, last * P)
+            if first == 0:
+                one = [look_up(EARLY, 0, first, last, "codes3"), look_up(EARLY + 1, 0, first, last, "late")]
+                two = look_up(EARLY, 1, first, last, None)
             else:
-                prepare_second()
-            one = sb([P, width], F32, "seen%d_0" % t, tag="stage%d" % (t + 1))
-            two = sb([P, width], F32, "seen%d_1" % t, tag="other%d" % t)
-            perceive(t, first, last, (one[:], two[:]))
-        done = list(range(first, last))
-        for c, tag in ((1, "other2"), (2, "rows0")):
-            for b in done:
-                turn_back(b)
-            first, last = CHUNKS[c]
-            seen = sb([P, 2 * TILES * P], F32, "seen_late%d" % c, tag=tag)
-            if c == 2:
-                for b in range(*CHUNKS[0]):
-                    finish(b)
-            for t in range(TILES):
-                perceive(t, first, last, [seen[:, (2 * t + n) * P : (2 * t + n + 1) * P] for n in range(2)])
-            done = list(range(first, last))
-        finish(2)
-        turn_back(3)
-        finish(3)
+                if first == 2:
+                    late = sb([P, 3 * P], F32, "seen_late", tag="late")
+                at = 2 * (first - 2)
+                one = [look_up(EARLY, 0, first, last, None, late[:, block(at)]), look_up(EARLY + 1, 0, first, last, None)]
+                if first == 2:
+                    two = look_up(EARLY, 1, first, last, None, late[:, block(1)])
+                else:
+                    two = look_up(EARLY, 1, first, last, "h_grouped0")
+            for b in range(first, last):
+                add_turned(high[b - first][:, block(0)], two[:, block(b, first)], start=True)
+            for t in range(EARLY, TILES):
+                own = sb([P, cols.stop - cols.start], F32, "own%d_%d" % (t, first))
+                nc.vector.tensor_tensor(own[:], one[t - EARLY], y[t][:, cols], ALU.add)
+                for b in range(first, last):
+                    add_turned(high[b - first][:, block(t, EARLY)], own[:, block(b, first)])
+            two = look_up(EARLY + 1, 1, first, last, None)
+            for b in range(first, last):
+                add_turned(high[b - first][:, block(1)], two[:, block(b, first)], stop=True)
+            for b in range(first, last):
+                rectify(b, 1, high[b - first][:])
+            grouped.append(turn_back(first, last))
+        update(*GROUPS[0], rr_first)
+        update(*GROUPS[1], second_product(*GROUPS[1], grouped[1], 1))
+        update(*GROUPS[2], second_product(*GROUPS[2], grouped[2], HALVES))

@@ -19,33 +19,45 @@ ACT = mybir.ActivationFunctionType
 P = 128
 PACK = 4
 PER_COL = 16
+QUADRANT = 32
+NEIGHBOURS = 2
 TILES = H // P
 BLOCKS = S // P
 HALVES = N // P
-GROUPS = ((0, 2), (2, 3), (3, 4))
-SPARE = 16
+BANKS = 8
 EARLY = 2
+SPARE = 16
+GROUPS = ((0, 2), (2, 3), (3, 4))
 
 
-def interleave(nc, grouped, raw):
-    nc.scalar.copy(
+def span(first, last=None):
+    return slice(first * P, (first + 1 if last is None else last) * P)
+
+
+def entries(offsets, cols):
+    return offsets[:, cols.start // PER_COL : cols.stop // PER_COL]
+
+
+def interleave(copy, grouped, raw):
+    copy(
         out=grouped.rearrange("p (c i t) -> p c t i", i=4, t=PACK),
         in_=raw.rearrange("p t (c i) -> p c t i", i=4),
     )
 
 
-def tile_picked_ynca_tanh_p_kernel(tc, x_words, x_scales, w1, w2, kern, cur, fire, offs, pos1, pos2, out):
+def tile_picked_ynca_tanh_p_kernel(
+    tc, x_words, x_scales, w1, w2, kern, cur, fire, offs, pos1, pos2, out
+):
     nc = tc.nc
     with ExitStack() as ctx:
         keep = ctx.enter_context(tc.tile_pool(name="keep", bufs=1))
-        ring = ctx.enter_context(tc.psum_pool(name="ring", bufs=7))
-        shared = ctx.enter_context(tc.psum_pool(name="shared", bufs=1))
+        ring = ctx.enter_context(tc.psum_pool(name="ring", bufs=BANKS - 1))
+        chain = ctx.enter_context(tc.psum_pool(name="chain", bufs=1))
 
         def sb(shape, dtype, name, tag=None):
             return keep.tile(shape, dtype, name=name, tag=tag or name, align_bytes=64)
 
-        def bank(shape, name):
-            pool = shared if name in ("y_acc3", "fire_turned", "h_turned0", "pre_high3", "rr2_0") else ring
+        def bank(shape, name, pool=ring):
             return pool.tile(shape, F32, name=name, tag="bank")
 
         scale_table = sb([P, T], U8, "scale_table")
@@ -59,27 +71,27 @@ def tile_picked_ynca_tanh_p_kernel(tc, x_words, x_scales, w1, w2, kern, cur, fir
         nc.scalar.activation(warm_out[:], warm[:], ACT.Tanh)
 
         w1_rows = w1.rearrange("(p t) c -> p t c", t=PACK)
-        w1_raw = [sb([P, PACK, P], F32, "w1_raw%d" % t) for t in range(2)]
-        w1_rest = sb([P, PACK, 2 * P], F32, "w1_rest")
+        w1_raw = [sb([P, PACK, P], F32, "w1_raw%d" % t) for t in range(EARLY)]
+        w1_rest = sb([P, PACK, (TILES - EARLY) * P], F32, "w1_rest")
         word_table = sb([P, T], U32, "word_table")
-        kern_sb = [sb([P, S], F32, "kern%d" % n) for n in range(2)]
-        pos_sb = [keep.tile([P, S // PER_COL], U16, name="pos%d" % n) for n in range(2)]
-        w2_raw = sb([P, PACK, N], F32, "w2_raw", tag="y3")
+        kern_sb = [sb([P, S], F32, "kern%d" % n) for n in range(NEIGHBOURS)]
+        pos_sb = [keep.tile([P, S // PER_COL], U16, name="pos%d" % n) for n in range(NEIGHBOURS)]
+        w2_raw = sb([P, PACK, N], F32, "w2_raw")
         fire_rows = sb([P, P], F32, "fire_rows")
         cur_sb = sb([P, HALVES, S], F32, "cur_sb")
 
-        nc.sync.dma_start(w1_raw[0][:], w1_rows[:, :, 0:P])
-        for q in range(4):
+        nc.sync.dma_start(w1_raw[0][:], w1_rows[:, :, span(0)])
+        for q in range(P // QUADRANT):
             nc.sync.dma_start(
-                scale_table[32 * q : 32 * q + 4, :].bitcast(I32), x_scales[0, 4 * q : 4 * q + 4, :].bitcast(I32)
+                scale_table[QUADRANT * q : QUADRANT * q + 4, :].bitcast(I32),
+                x_scales[0, 4 * q : 4 * q + 4, :].bitcast(I32),
             )
         nc.sync.dma_start(word_table[:].bitcast(I32), x_words[0].rearrange("p n t -> p (n t)").bitcast(I32))
-        nc.sync.dma_start(w1_raw[1][:], w1_rows[:, :, P : 2 * P])
-        nc.sync.dma_start(pos_sb[0][:], pos1)
-        nc.sync.dma_start(kern_sb[0][:], kern[0])
-        nc.sync.dma_start(pos_sb[1][:], pos2)
-        nc.sync.dma_start(kern_sb[1][:], kern[1])
-        nc.sync.dma_start(w1_rest[:], w1_rows[:, :, 2 * P :])
+        nc.sync.dma_start(w1_raw[1][:], w1_rows[:, :, span(1)])
+        for n, pos in enumerate((pos1, pos2)):
+            nc.sync.dma_start(pos_sb[n][:], pos)
+            nc.sync.dma_start(kern_sb[n][:], kern[n])
+        nc.sync.dma_start(w1_rest[:], w1_rows[:, :, span(EARLY, TILES)])
         nc.sync.dma_start(fire_rows[:], fire[0 : P // BLOCKS, :].rearrange("r (b j) -> (r b) j", j=P))
         nc.sync.dma_start(w2_raw[:], w2.rearrange("(p t) c -> p t c", t=PACK))
         nc.sync.dma_start(cur_sb[:], cur.rearrange("(h p) j -> p h j", p=P))
@@ -90,13 +102,13 @@ def tile_picked_ynca_tanh_p_kernel(tc, x_words, x_scales, w1, w2, kern, cur, fir
         x_scale = sb([P, S], U8, "x_scale")
         nc.vector.tensor_copy(x_scale[:], scale_table[:].indirect(offs_sb[:]))
 
-        w1_views = [w1_raw[0][:], w1_raw[1][:], w1_rest[:, :, 0:P], w1_rest[:, :, P:]]
-        w1_codes = [sb([P, P], U32, "w1_codes%d" % t, tag="codes%d" % t) for t in range(TILES)]
+        w1_views = [raw[:] for raw in w1_raw] + [w1_rest[:, :, span(t)] for t in range(TILES - EARLY)]
+        w1_codes = [sb([P, P], U32, "w1_codes%d" % t) for t in range(TILES)]
         w1_scale = [sb([P, P], U8, "w1_scale%d" % t) for t in range(TILES)]
 
-        def quantise_w1(t):
-            grouped = sb([P, P * PACK], BF16, "w1_grouped%d" % t, tag="stage%d" % t)
-            interleave(nc, grouped[:], w1_views[t])
+        def quantise_w1(t, copy):
+            grouped = sb([P, P * PACK], BF16, "w1_grouped%d" % t)
+            interleave(copy, grouped[:], w1_views[t])
             nc.vector.quantize_mx(out=w1_codes[t][:].bitcast(FP8X4), scales=w1_scale[t][:], in_=grouped[:])
 
         x_codes = sb([P, S], U32, "x_codes")
@@ -104,8 +116,8 @@ def tile_picked_ynca_tanh_p_kernel(tc, x_words, x_scales, w1, w2, kern, cur, fir
         for t in range(EARLY):
             nc.gpsimd.memset(y[t][:, S:], 0.0)
 
-        def first_product(t, cols, name):
-            acc = bank([P, cols.stop - cols.start], name)
+        def first_product(t, cols, name, pool=ring):
+            acc = bank([P, cols.stop - cols.start], name, pool)
             nc.tensor.matmul_mx(
                 out=acc[:],
                 lhsT=w1_codes[t][:].bitcast(FP8X4),
@@ -117,56 +129,39 @@ def tile_picked_ynca_tanh_p_kernel(tc, x_words, x_scales, w1, w2, kern, cur, fir
             )
             return acc
 
-        quantise_w1(0)
-        half = S // 2
-        for a in range(2):
-            cols = slice(a * half, (a + 1) * half)
-            nc.vector.tensor_copy(
-                x_codes[:, cols], word_table[:].indirect(offs_sb[:, cols.start // PER_COL : cols.stop // PER_COL])
-            )
-        acc = first_product(0, slice(0, half), "y0_low")
-        nc.scalar.copy(y[0][:, 0:half], acc[:])
-        acc = first_product(0, slice(half, S), "y0_high")
-        nc.scalar.copy(y[0][:, half:S], acc[:])
-
-        def make_y(t):
-            quantise_w1(t)
-            acc = first_product(t, slice(0, S), "y_acc%d" % t)
-            if t == TILES - 1:
-                interleave(nc, w2_grouped[:], w2_raw[:])
-                y.append(sb([P, S], F32, "y%d" % t))
-            nc.scalar.copy(y[t][:, 0:S], acc[:])
+        quantise_w1(0, nc.scalar.copy)
+        cell_halves = (span(0, BLOCKS // 2), span(BLOCKS // 2, BLOCKS))
+        for cols in cell_halves:
+            nc.vector.tensor_copy(x_codes[:, cols], word_table[:].indirect(entries(offs_sb, cols)))
+        for cols in cell_halves:
+            acc = first_product(0, cols, "y_acc0_%d" % cols.start)
+            nc.scalar.copy(y[0][:, cols], acc[:])
 
         fire_col = sb([P, BLOCKS], F32, "fire_col")
         w2_codes = sb([P, N], U32, "w2_codes")
         w2_scale = sb([P, N], U8, "w2_scale")
+        w2_grouped = sb([P, N * PACK], BF16, "w2_grouped")
+        h_rows = [sb([P, H], BF16, "h_rows%d" % b) for b in range(BLOCKS)]
+        all_cells = span(0, BLOCKS)
 
-        def look_up(t, n, first, last, tag, seen=None):
-            cols = slice(first * P, last * P)
-            if seen is None:
-                seen = sb([P, cols.stop - cols.start], F32, "seen%d_%d_%d" % (t, n, first), tag=tag)[:]
-            nc.vector.tensor_tensor(
-                seen,
-                y[t][:].indirect(pos_sb[n][:, cols.start // PER_COL : cols.stop // PER_COL]),
-                kern_sb[n][:, cols],
-                ALU.mult,
-            )
-            return seen
+        def make_y(t, copy):
+            quantise_w1(t, copy)
+            acc = first_product(t, all_cells, "y_acc%d" % t)
+            nc.scalar.copy(y[t][:, all_cells], acc[:])
+
+        def make_last_y():
+            t = TILES - 1
+            quantise_w1(t, nc.scalar.copy)
+            acc = first_product(t, all_cells, "y_acc%d" % t, chain)
+            interleave(nc.scalar.copy, w2_grouped[:], w2_raw[:])
+            y.append(sb([P, S], F32, "y%d" % t, tag="w2_raw"))
+            nc.scalar.copy(y[t][:], acc[:])
+
+        def look_up(t, n, cols, seen):
+            nc.vector.tensor_tensor(seen, y[t][:].indirect(entries(pos_sb[n], cols)), kern_sb[n][:, cols], ALU.mult)
 
         def add_turned(target, term, start=False, stop=False):
             nc.tensor.matmul(target, term, ident[:], start=start, stop=stop, is_transpose=True)
-
-        def block(b, first=0):
-            return slice((b - first) * P, (b - first + 1) * P)
-
-        w2_grouped = sb([P, N * PACK], BF16, "w2_grouped")
-
-        def prepare_second():
-            turned = bank([P, P], "fire_turned")
-            nc.tensor.transpose(turned[:], fire_rows[:], ident[:])
-            nc.scalar.copy(fire_col[:], turned[:, 0:BLOCKS])
-
-        h_rows = [sb([P, H], BF16, "h_rows%d" % b) for b in range(BLOCKS)]
 
         def rectify(b, part, pre):
             rows = h_rows[b][:].rearrange("j (u p e) -> j u p e", u=2, e=2)
@@ -181,30 +176,28 @@ def tile_picked_ynca_tanh_p_kernel(tc, x_words, x_scales, w1, w2, kern, cur, fir
             grouped = sb([P, (last - first) * P * PACK], BF16, "h_grouped%d" % first)
             words = grouped[:].bitcast(F32)
             for b in range(first, last):
-                turned = bank([P, 2, P], "h_turned%d" % b)
+                turned = bank([P, 2, P], "h_turned%d" % b, chain if b == 0 else ring)
                 pairs = h_rows[b][:].bitcast(F32)
                 for u in range(2):
-                    nc.tensor.transpose(turned[:, u, :], pairs[:, block(u)], ident[:])
+                    nc.tensor.transpose(turned[:, u, :], pairs[:, span(u)], ident[:])
                 nc.scalar.copy(
-                    words[:, 2 * P * (b - first) : 2 * P * (b - first + 1)].rearrange("p (j u) -> p j u", u=2),
+                    words[:, span(2 * (b - first), 2 * (b - first + 1))].rearrange("p (j u) -> p j u", u=2),
                     turned[:].rearrange("p u j -> p j u"),
                 )
             return grouped
 
-        out_rows = out.rearrange("(h p) j -> p h j", p=P)
-
-        def second_product(first, last, grouped, parts):
+        def second_product(first, last, grouped, parts, pool=ring):
             width = (last - first) * P
             h_codes = sb([P, width], U32, "h_codes%d" % first)
             h_scale = sb([P, width], U8, "h_scale%d" % first)
             nc.vector.quantize_mx(out=h_codes[:].bitcast(FP8X4), scales=h_scale[:], in_=grouped[:])
             per = HALVES // parts
-            rr = [bank([P, per, width], "rr%d_%d" % (first, i)) for i in range(parts)]
-            for h in range(HALVES):
+            rr = [bank([P, per, width], "rr%d_%d" % (first, i), pool) for i in range(parts)]
+            for m in range(HALVES):
                 nc.tensor.matmul_mx(
-                    out=rr[h // per][:, h % per, :],
-                    lhsT=w2_codes[:, h * P : (h + 1) * P].bitcast(FP8X4),
-                    lhsT_scale=w2_scale[:, h * P : (h + 1) * P],
+                    out=rr[m // per][:, m % per, :],
+                    lhsT=w2_codes[:, span(m)].bitcast(FP8X4),
+                    lhsT_scale=w2_scale[:, span(m)],
                     rhs=h_codes[:].bitcast(FP8X4),
                     rhs_scale=h_scale[:],
                     start=True,
@@ -212,66 +205,72 @@ def tile_picked_ynca_tanh_p_kernel(tc, x_words, x_scales, w1, w2, kern, cur, fir
                 )
             return rr
 
-        def update(first, last, rr):
-            cols = slice(first * P, last * P)
+        out_rows = out.rearrange("(m p) j -> p m j", p=P)
+
+        def update(first, last, rr, tag=None):
+            cols = span(first, last)
             per = HALVES // len(rr)
-            for i, part in enumerate(rr):
+            for i, acc in enumerate(rr):
                 rows = slice(i * per, (i + 1) * per)
-                moved = sb([P, per, cols.stop - cols.start], F32, "moved%d_%d" % (first, i))
-                nc.vector.tensor_tensor(moved[:], part[:], cur_sb[:, rows, cols], ALU.add)
-                state = sb([P, per, cols.stop - cols.start], F32, "state%d_%d" % (first, i), tag="fire_col" if first == 0 else None)
+                shape = [P, per, cols.stop - cols.start]
+                moved = sb(shape, F32, "moved%d_%d" % (first, i))
+                nc.vector.tensor_tensor(moved[:], acc[:], cur_sb[:, rows, cols], ALU.add)
+                state = sb(shape, F32, "state%d_%d" % (first, i), tag=tag)
                 nc.scalar.activation(state[:], moved[:], ACT.Tanh)
                 nc.sync.dma_start(out_rows[:, rows, cols], state[:])
 
         low = [bank([P, 2, EARLY * P], "pre_low%d" % i) for i in range(BLOCKS // 2)]
-        make_y(1)
-        tags = (("stage1", "free0"), ("stage2", "stage3"))
+        make_y(1, nc.vector.tensor_copy)
+        slots = (("w1_grouped1", None), ("w1_grouped2", "w1_grouped3"))
         for t in range(EARLY):
-            if t == 1:
-                make_y(2)
-                make_y(3)
+            if t == EARLY - 1:
+                make_y(EARLY, nc.scalar.copy)
+                make_last_y()
             for b in range(BLOCKS):
-                add_turned(low[b // 2][:, b % 2, block(t)], y[t][:, block(b)], start=(t == 0 and b % 2 == 0))
-            for n in range(2):
-                seen = look_up(t, n, 0, BLOCKS, tags[t][n])
+                add_turned(low[b // 2][:, b % 2, span(t)], y[t][:, span(b)], start=(t == 0 and b % 2 == 0))
+            for n in range(NEIGHBOURS):
+                seen = sb([P, S], F32, "seen%d_%d" % (t, n), tag=slots[t][n])
+                look_up(t, n, all_cells, seen[:])
                 for b in range(BLOCKS):
-                    closing = t == EARLY - 1 and n == 1 and b % 2 == 1
-                    add_turned(low[b // 2][:, b % 2, block(t)], seen[:, block(b)], stop=closing)
-        prepare_second()
+                    closing = t == EARLY - 1 and n == NEIGHBOURS - 1 and b % 2 == 1
+                    add_turned(low[b // 2][:, b % 2, span(t)], seen[:, span(b)], stop=closing)
+
+        fire_turned = bank([P, P], "fire_turned", chain)
+        nc.tensor.transpose(fire_turned[:], fire_rows[:], ident[:])
+        nc.scalar.copy(fire_col[:], fire_turned[:, 0:BLOCKS])
         for b in range(BLOCKS):
             rectify(b, 0, low[b // 2][:, b % 2, :])
+        nc.vector.quantize_mx(out=w2_codes[:].bitcast(FP8X4), scales=w2_scale[:], in_=w2_grouped[:])
+
         grouped = []
         for first, last in GROUPS:
-            if first == GROUPS[-1][0]:
-                nc.vector.quantize_mx(out=w2_codes[:].bitcast(FP8X4), scales=w2_scale[:], in_=w2_grouped[:])
-                rr_first = second_product(*GROUPS[0], grouped[0], 1)
-            high = [bank([P, (TILES - EARLY) * P], "pre_high%d" % b) for b in range(first, last)]
-            cols = slice(first * P, last * P)
-            if first == 0:
-                one = [look_up(EARLY, 0, first, last, "codes3"), look_up(EARLY + 1, 0, first, last, "late")]
-                two = look_up(EARLY, 1, first, last, None)
-            else:
-                if first == 2:
-                    late = sb([P, 3 * P], F32, "seen_late", tag="late")
-                at = 2 * (first - 2)
-                one = [look_up(EARLY, 0, first, last, None, late[:, block(at)]), look_up(EARLY + 1, 0, first, last, None)]
-                if first == 2:
-                    two = look_up(EARLY, 1, first, last, None, late[:, block(1)])
-                else:
-                    two = look_up(EARLY, 1, first, last, "h_grouped0")
-            for b in range(first, last):
-                add_turned(high[b - first][:, block(0)], two[:, block(b, first)], start=True)
+            cols = span(first, last)
+            high = [
+                bank([P, (TILES - EARLY) * P], "pre_high%d" % b, chain if b == BLOCKS - 1 else ring)
+                for b in range(first, last)
+            ]
             for t in range(EARLY, TILES):
-                own = sb([P, cols.stop - cols.start], F32, "own%d_%d" % (t, first))
-                nc.vector.tensor_tensor(own[:], one[t - EARLY], y[t][:, cols], ALU.add)
                 for b in range(first, last):
-                    add_turned(high[b - first][:, block(t, EARLY)], own[:, block(b, first)])
-            two = look_up(EARLY + 1, 1, first, last, None)
-            for b in range(first, last):
-                add_turned(high[b - first][:, block(1)], two[:, block(b, first)], stop=True)
+                    add_turned(high[b - first][:, span(t - EARLY)], y[t][:, span(b)], start=(t == EARLY))
+            if first == GROUPS[1][0]:
+                held = sb([P, NEIGHBOURS * (BLOCKS - first) * P], F32, "seen_held", tag="fire_rows")
+            for t in range(EARLY, TILES):
+                for n in range(NEIGHBOURS):
+                    if t == EARLY and first > 0:
+                        seen = held[:, span(NEIGHBOURS * (first - GROUPS[1][0]) + n)]
+                    else:
+                        tag = "w1_codes%d" % (TILES - 1) if (t, n) == (EARLY, 0) else None
+                        seen = sb([P, cols.stop - cols.start], F32, "seen%d_%d_%d" % (t, n, first), tag=tag)[:]
+                    look_up(t, n, cols, seen)
+                    for b in range(first, last):
+                        closing = t == TILES - 1 and n == NEIGHBOURS - 1
+                        add_turned(high[b - first][:, span(t - EARLY)], seen[:, span(b - first)], stop=closing)
+            if last == BLOCKS:
+                rr_first = second_product(*GROUPS[0], grouped[0], 1)
             for b in range(first, last):
                 rectify(b, 1, high[b - first][:])
             grouped.append(turn_back(first, last))
-        update(*GROUPS[0], rr_first)
-        update(*GROUPS[1], second_product(*GROUPS[1], grouped[1], 1))
+
+        update(*GROUPS[0], rr_first, tag="fire_col")
+        update(*GROUPS[1], second_product(*GROUPS[1], grouped[1], 1, chain))
         update(*GROUPS[2], second_product(*GROUPS[2], grouped[2], HALVES))

@@ -67,7 +67,6 @@ def tile_picked_ynca_tanh_p_kernel(
         nc.vector.memset(warm[:], 0.0)
 
         offs_sb = keep.tile([P, S // PER_COL], U16, name="offs_sb")
-        nc.sync.dma_start(offs_sb[:], offs)
         nc.scalar.activation(warm_out[:], warm[:], ACT.Tanh)
 
         w1_rows = w1.rearrange("(p t) c -> p t c", t=PACK)
@@ -81,6 +80,7 @@ def tile_picked_ynca_tanh_p_kernel(
         cur_sb = sb([P, HALVES, S], F32, "cur_sb")
 
         nc.sync.dma_start(w1_raw[0][:], w1_rows[:, :, span(0)])
+        nc.sync.dma_start(offs_sb[:], offs)
         for q in range(P // QUADRANT):
             nc.sync.dma_start(
                 scale_table[QUADRANT * q : QUADRANT * q + 4, :].bitcast(I32),
@@ -133,7 +133,7 @@ def tile_picked_ynca_tanh_p_kernel(
         cell_halves = (span(0, BLOCKS // 2), span(BLOCKS // 2, BLOCKS))
         for cols in cell_halves:
             nc.vector.tensor_copy(x_codes[:, cols], word_table[:].indirect(entries(offs_sb, cols)))
-        for cols in cell_halves:
+        for cols in [cell_halves[0]] + [span(b) for b in range(BLOCKS // 2, BLOCKS)]:
             acc = first_product(0, cols, "y_acc0_%d" % cols.start)
             nc.scalar.copy(y[0][:, cols], acc[:])
 

@@ -81,12 +81,11 @@ def tile_picked_ynca_tanh_p_kernel(
 
         nc.sync.dma_start(w1_raw[0][:], w1_rows[:, :, span(0)])
         nc.sync.dma_start(offs_sb[:], offs)
-        for q in range(P // QUADRANT):
-            nc.sync.dma_start(
-                scale_table[QUADRANT * q : QUADRANT * q + 4, :].bitcast(I32),
-                x_scales[0, 4 * q : 4 * q + 4, :].bitcast(I32),
-            )
-        nc.sync.dma_start(word_table[:].bitcast(I32), x_words[0].rearrange("p n t -> p (n t)").bitcast(I32))
+        word_rows = x_words[0].rearrange("p n t -> p (n t)").bitcast(I32)
+        nc.sync.dma_start(word_table[:, : T // 4].bitcast(I32), word_rows[:, : T // 4])
+        for r in range(4):
+            nc.sync.dma_start(scale_table[r:P:QUADRANT, :].bitcast(I32), x_scales[0, r::4, :].bitcast(I32))
+        nc.sync.dma_start(word_table[:, T // 4 :].bitcast(I32), word_rows[:, T // 4 :])
         nc.sync.dma_start(w1_raw[1][:], w1_rows[:, :, span(1)])
         for n, pos in enumerate((pos1, pos2)):
             nc.sync.dma_start(pos_sb[n][:], pos)
@@ -138,7 +137,6 @@ def tile_picked_ynca_tanh_p_kernel(
             nc.scalar.copy(y[0][:, cols], acc[:])
 
         fire_col = sb([P, BLOCKS], F32, "fire_col")
-        w2_codes = sb([P, N], U32, "w2_codes")
         w2_scale = sb([P, N], U8, "w2_scale")
         w2_grouped = sb([P, N * PACK], BF16, "w2_grouped")
         h_rows = [sb([P, H], BF16, "h_rows%d" % b) for b in range(BLOCKS)]
@@ -240,7 +238,6 @@ def tile_picked_ynca_tanh_p_kernel(
         nc.scalar.copy(fire_col[:], fire_turned[:, 0:BLOCKS])
         for b in range(BLOCKS):
             rectify(b, 0, low[b // 2][:, b % 2, :])
-        nc.vector.quantize_mx(out=w2_codes[:].bitcast(FP8X4), scales=w2_scale[:], in_=w2_grouped[:])
 
         grouped = []
         for first, last in GROUPS:
@@ -266,6 +263,8 @@ def tile_picked_ynca_tanh_p_kernel(
                         closing = t == TILES - 1 and n == NEIGHBOURS - 1
                         add_turned(high[b - first][:, span(t - EARLY)], seen[:, span(b - first)], stop=closing)
             if last == BLOCKS:
+                w2_codes = sb([P, N], U32, "w2_codes", tag="w2_raw")
+                nc.vector.quantize_mx(out=w2_codes[:].bitcast(FP8X4), scales=w2_scale[:], in_=w2_grouped[:])
                 rr_first = second_product(*GROUPS[0], grouped[0], 1)
             for b in range(first, last):
                 rectify(b, 1, high[b - first][:])

@@ -205,17 +205,17 @@ def tile_picked_ynca_tanh_p_kernel(
 
         out_rows = out.rearrange("(m p) j -> p m j", p=P)
 
-        def update(first, last, rr, tag=None):
+        def update(first, last, rr, i, moved_tag=None, state=None):
             cols = span(first, last)
             per = HALVES // len(rr)
-            for i, acc in enumerate(rr):
-                rows = slice(i * per, (i + 1) * per)
-                shape = [P, per, cols.stop - cols.start]
-                moved = sb(shape, F32, "moved%d_%d" % (first, i))
-                nc.vector.tensor_tensor(moved[:], acc[:], cur_sb[:, rows, cols], ALU.add)
-                state = sb(shape, F32, "state%d_%d" % (first, i), tag=tag)
-                nc.scalar.activation(state[:], moved[:], ACT.Tanh)
-                nc.sync.dma_start(out_rows[:, rows, cols], state[:])
+            rows = slice(i * per, (i + 1) * per)
+            shape = [P, per, cols.stop - cols.start]
+            moved = sb(shape, F32, "moved%d_%d" % (first, i), tag=moved_tag)
+            nc.vector.tensor_tensor(moved[:], rr[i][:], cur_sb[:, rows, cols], ALU.add)
+            if state is None:
+                state = sb(shape, F32, "state%d_%d" % (first, i))[:]
+            nc.scalar.activation(state, moved[:], ACT.Tanh)
+            nc.sync.dma_start(out_rows[:, rows, cols], state)
 
         low = [bank([P, 2, EARLY * P], "pre_low%d" % i) for i in range(BLOCKS // 2)]
         make_y(1, nc.vector.tensor_copy)
@@ -251,25 +251,33 @@ def tile_picked_ynca_tanh_p_kernel(
                     add_turned(high[b - first][:, span(t - EARLY)], y[t][:, span(b)], start=(t == EARLY))
             if first == GROUPS[1][0]:
                 held = sb([P, NEIGHBOURS * (BLOCKS - first) * P], F32, "seen_held", tag="fire_rows")
-            for t in range(EARLY, TILES):
+            for n in range(NEIGHBOURS):
+                if first > 0:
+                    seen = held[:, span(NEIGHBOURS * (first - GROUPS[1][0]) + n)]
+                else:
+                    tag = "w1_codes%d" % (TILES - 1) if n == 0 else None
+                    seen = sb([P, cols.stop - cols.start], F32, "seen%d_%d_%d" % (EARLY, n, first), tag=tag)[:]
+                look_up(EARLY, n, cols, seen)
+                for b in range(first, last):
+                    add_turned(high[b - first][:, span(0)], seen[:, span(b - first)])
+            for b in range(first, last):
                 for n in range(NEIGHBOURS):
-                    if t == EARLY and first > 0:
-                        seen = held[:, span(NEIGHBOURS * (first - GROUPS[1][0]) + n)]
-                    else:
-                        tag = "w1_codes%d" % (TILES - 1) if (t, n) == (EARLY, 0) else None
-                        seen = sb([P, cols.stop - cols.start], F32, "seen%d_%d_%d" % (t, n, first), tag=tag)[:]
-                    look_up(t, n, cols, seen)
-                    for b in range(first, last):
-                        closing = t == TILES - 1 and n == NEIGHBOURS - 1
-                        add_turned(high[b - first][:, span(t - EARLY)], seen[:, span(b - first)], stop=closing)
+                    seen = sb([P, P], F32, "seen%d_%d_%d" % (TILES - 1, n, b))
+                    look_up(TILES - 1, n, span(b), seen[:])
+                    add_turned(high[b - first][:, span(1)], seen[:], stop=(n == NEIGHBOURS - 1))
             if last == BLOCKS:
                 w2_codes = sb([P, N], U32, "w2_codes", tag="w2_raw")
                 nc.vector.quantize_mx(out=w2_codes[:].bitcast(FP8X4), scales=w2_scale[:], in_=w2_grouped[:])
-                rr_first = second_product(*GROUPS[0], grouped[0], 1)
+                rr_first = second_product(*GROUPS[0], grouped[0], HALVES)
             for b in range(first, last):
                 rectify(b, 1, high[b - first][:])
             grouped.append(turn_back(first, last))
 
-        update(*GROUPS[0], rr_first, tag="fire_col")
-        update(*GROUPS[1], second_product(*GROUPS[1], grouped[1], 1, chain))
-        update(*GROUPS[2], second_product(*GROUPS[2], grouped[2], HALVES))
+        state_first = sb([P, HALVES, 2 * P], F32, "state_first", tag="h_rows3")
+        update(*GROUPS[0], rr_first, 0, state=state_first[:, 0:1, :])
+        rr_second = second_product(*GROUPS[1], grouped[1], 1, chain)
+        update(*GROUPS[0], rr_first, 1, moved_tag="h_grouped%d" % GROUPS[1][0], state=state_first[:, 1:2, :])
+        rr_last = second_product(*GROUPS[2], grouped[2], HALVES)
+        update(*GROUPS[1], rr_second, 0, moved_tag="h_grouped%d" % GROUPS[2][0])
+        for i in range(HALVES):
+            update(*GROUPS[2], rr_last, i)

@@ -51,8 +51,9 @@ def tile_picked_ynca_tanh_p_kernel(
     nc = tc.nc
     with ExitStack() as ctx:
         keep = ctx.enter_context(tc.tile_pool(name="keep", bufs=1))
-        ring = ctx.enter_context(tc.psum_pool(name="ring", bufs=BANKS - 1))
+        ring = ctx.enter_context(tc.psum_pool(name="ring", bufs=BANKS - 2))
         chain = ctx.enter_context(tc.psum_pool(name="chain", bufs=1))
+        chain2 = ctx.enter_context(tc.psum_pool(name="chain2", bufs=1))
 
         def sb(shape, dtype, name, tag=None):
             return keep.tile(shape, dtype, name=name, tag=tag or name, align_bytes=64)
@@ -75,7 +76,7 @@ def tile_picked_ynca_tanh_p_kernel(
         word_table = sb([P, T], U32, "word_table")
         kern_sb = [sb([P, S], F32, "kern%d" % n) for n in range(NEIGHBOURS)]
         pos_sb = [keep.tile([P, S // PER_COL], U16, name="pos%d" % n) for n in range(NEIGHBOURS)]
-        w2_raw = sb([P, PACK, N], F32, "w2_raw")
+        w2_raw = [sb([P, PACK, P], F32, "w2_raw%d" % m) for m in range(HALVES)]
         fire_rows = sb([P, P], F32, "fire_rows")
         cur_sb = sb([P, HALVES, S], F32, "cur_sb")
 
@@ -91,8 +92,9 @@ def tile_picked_ynca_tanh_p_kernel(
             nc.sync.dma_start(pos_sb[n][:], pos)
             nc.sync.dma_start(kern_sb[n][:], kern[n])
         nc.sync.dma_start(w1_rest[:], w1_rows[:, :, span(EARLY, TILES)])
+        for m in range(HALVES):
+            nc.sync.dma_start(w2_raw[m][:], w2.rearrange("(p t) c -> p t c", t=PACK)[:, :, span(m)])
         nc.sync.dma_start(fire_rows[:], fire[0 : P // BLOCKS, :].rearrange("r (b j) -> (r b) j", j=P))
-        nc.sync.dma_start(w2_raw[:], w2.rearrange("(p t) c -> p t c", t=PACK))
         nc.sync.dma_start(cur_sb[:], cur.rearrange("(h p) j -> p h j", p=P))
 
         ident = sb([P, P], F32, "ident")
@@ -111,9 +113,8 @@ def tile_picked_ynca_tanh_p_kernel(
             nc.vector.quantize_mx(out=w1_codes[t][:].bitcast(FP8X4), scales=w1_scale[t][:], in_=grouped[:])
 
         x_codes = sb([P, S], U32, "x_codes")
-        y = [sb([P, S + SPARE if t < EARLY else S], F32, "y%d" % t) for t in range(TILES - 1)]
-        for t in range(EARLY):
-            nc.gpsimd.memset(y[t][:, S:], 0.0)
+        y = [sb([P, S + SPARE if t == 0 else S], F32, "y%d" % t) for t in range(EARLY)]
+        nc.gpsimd.memset(y[0][:, S:], 0.0)
 
         def first_product(t, cols, name, pool=ring):
             acc = bank([P, cols.stop - cols.start], name, pool)
@@ -145,14 +146,17 @@ def tile_picked_ynca_tanh_p_kernel(
         def make_y(t, copy):
             quantise_w1(t, copy)
             acc = first_product(t, all_cells, "y_acc%d" % t)
+            if t == EARLY:
+                for m in range(HALVES):
+                    interleave(nc.scalar.copy, w2_grouped[:, span(PACK * m, PACK * (m + 1))], w2_raw[m][:])
+                y.append(sb([P, S], F32, "y%d" % t, tag="w2_raw0"))
             nc.scalar.copy(y[t][:, all_cells], acc[:])
 
         def make_last_y():
             t = TILES - 1
             quantise_w1(t, nc.scalar.copy)
             acc = first_product(t, all_cells, "y_acc%d" % t, chain)
-            interleave(nc.scalar.copy, w2_grouped[:], w2_raw[:])
-            y.append(sb([P, S], F32, "y%d" % t, tag="w2_raw"))
+            y.append(sb([P, S], F32, "y%d" % t, tag="w2_raw1"))
             nc.scalar.copy(y[t][:], acc[:])
 
         def look_up(t, n, cols, seen):
@@ -161,10 +165,10 @@ def tile_picked_ynca_tanh_p_kernel(
         def add_turned(target, term, start=False, stop=False):
             nc.tensor.matmul(target, term, ident[:], start=start, stop=stop, is_transpose=True)
 
-        def rectify(b, part, pre):
+        def rectify(b, tiles, pre):
             rows = h_rows[b][:].rearrange("j (u p e) -> j u p e", u=2, e=2)
             nc.scalar.activation(
-                rows[:, :, part * (P // 2) : (part + 1) * (P // 2), :],
+                rows[:, :, tiles.start * (P // PACK) : tiles.stop * (P // PACK), :],
                 pre.rearrange("j (p u e) -> j u p e", u=2, e=2),
                 ACT.Relu,
                 scale=fire_col[:, b : b + 1],
@@ -184,11 +188,22 @@ def tile_picked_ynca_tanh_p_kernel(
                 )
             return grouped
 
-        def second_product(first, last, grouped, parts, pool=ring):
+        def quantise_w2(m):
+            nc.vector.quantize_mx(
+                out=w2_codes[:, span(m)].bitcast(FP8X4),
+                scales=w2_scale[:, span(m)],
+                in_=w2_grouped[:, span(PACK * m, PACK * (m + 1))],
+            )
+
+        def second_product(first, last, grouped, parts, pool=ring, with_weights=False):
             width = (last - first) * P
             h_codes = sb([P, width], U32, "h_codes%d" % first)
             h_scale = sb([P, width], U8, "h_scale%d" % first)
+            if with_weights:
+                quantise_w2(0)
             nc.vector.quantize_mx(out=h_codes[:].bitcast(FP8X4), scales=h_scale[:], in_=grouped[:])
+            if with_weights:
+                quantise_w2(1)
             per = HALVES // parts
             rr = [bank([P, per, width], "rr%d_%d" % (first, i), pool) for i in range(parts)]
             for m in range(HALVES):
@@ -221,61 +236,75 @@ def tile_picked_ynca_tanh_p_kernel(
         make_y(1, nc.vector.tensor_copy)
         slots = (("w1_grouped1", None), ("w1_grouped2", "w1_grouped3"))
         for t in range(EARLY):
+            for b in range(BLOCKS - t):
+                add_turned(low[b // 2][:, b % 2, span(t)], y[t][:, span(b)], start=(t == 0 and b % 2 == 0))
+        for t in range(EARLY):
             if t == EARLY - 1:
                 make_y(EARLY, nc.scalar.copy)
                 make_last_y()
-            for b in range(BLOCKS):
-                add_turned(low[b // 2][:, b % 2, span(t)], y[t][:, span(b)], start=(t == 0 and b % 2 == 0))
+            blocks = BLOCKS - t
             for n in range(NEIGHBOURS):
-                seen = sb([P, S], F32, "seen%d_%d" % (t, n), tag=slots[t][n])
-                look_up(t, n, all_cells, seen[:])
-                for b in range(BLOCKS):
-                    closing = t == EARLY - 1 and n == NEIGHBOURS - 1 and b % 2 == 1
+                seen = sb([P, blocks * P], F32, "seen%d_%d" % (t, n), tag=slots[t][n])
+                look_up(t, n, span(0, blocks), seen[:])
+                for b in range(blocks):
+                    closing = t == EARLY - 1 and n == NEIGHBOURS - 1 and b > 0
                     add_turned(low[b // 2][:, b % 2, span(t)], seen[:, span(b)], stop=closing)
 
         fire_turned = bank([P, P], "fire_turned", chain)
         nc.tensor.transpose(fire_turned[:], fire_rows[:], ident[:])
         nc.scalar.copy(fire_col[:], fire_turned[:, 0:BLOCKS])
         for b in range(BLOCKS):
-            rectify(b, 0, low[b // 2][:, b % 2, :])
+            tiles = 1 if b == BLOCKS - 1 else EARLY
+            rectify(b, range(tiles), low[b // 2][:, b % 2, span(0, tiles)])
 
         grouped = []
+        LAST = BLOCKS - 1
         for first, last in GROUPS:
             cols = span(first, last)
-            high = [
-                bank([P, (TILES - EARLY) * P], "pre_high%d" % b, chain if b == BLOCKS - 1 else ring)
-                for b in range(first, last)
-            ]
-            for t in range(EARLY, TILES):
+            tiles = range(1 if first == LAST else EARLY, TILES)
+            if first == LAST:
+                middle = bank([P, 2 * P], "pre_middle", chain)
+                final = bank([P, P], "pre_final", chain2)
+                sums = [{1: middle[:, span(0)], 2: middle[:, span(1)], 3: final[:]}]
+            else:
+                high = [bank([P, 2 * P], "pre_high%d" % b, chain2 if first else ring) for b in range(first, last)]
+                sums = [{t: acc[:, span(t - EARLY)] for t in tiles} for acc in high]
+            for t in tiles:
                 for b in range(first, last):
-                    add_turned(high[b - first][:, span(t - EARLY)], y[t][:, span(b)], start=(t == EARLY))
+                    opening = t == tiles.start or (b, t) == (LAST, TILES - 1)
+                    add_turned(sums[b - first][t], y[t][:, span(b)], start=opening)
             if first == GROUPS[1][0]:
-                held = sb([P, NEIGHBOURS * (BLOCKS - first) * P], F32, "seen_held", tag="fire_rows")
-            for n in range(NEIGHBOURS):
-                if first > 0:
-                    seen = held[:, span(NEIGHBOURS * (first - GROUPS[1][0]) + n)]
-                else:
-                    tag = "w1_codes%d" % (TILES - 1) if n == 0 else None
-                    seen = sb([P, cols.stop - cols.start], F32, "seen%d_%d_%d" % (EARLY, n, first), tag=tag)[:]
-                look_up(EARLY, n, cols, seen)
-                for b in range(first, last):
-                    add_turned(high[b - first][:, span(0)], seen[:, span(b - first)])
+                held = sb([P, 3 * NEIGHBOURS, P], F32, "seen_held", tag="fire_rows")
+            for t in tiles[:-1]:
+                for n in range(NEIGHBOURS):
+                    if first > 0:
+                        seen = held[:, NEIGHBOURS * (t if first == LAST else 0) + n, :]
+                    else:
+                        tag = "w1_codes%d" % (TILES - 1) if n == 0 else None
+                        seen = sb([P, cols.stop - cols.start], F32, "seen%d_%d_%d" % (t, n, first), tag=tag)[:]
+                    look_up(t, n, cols, seen)
+                    for b in range(first, last):
+                        closing = (b, t, n) == (LAST, TILES - 2, NEIGHBOURS - 1)
+                        add_turned(sums[b - first][t], seen[:, span(b - first)], stop=closing)
+            if first == LAST:
+                rectify(LAST, range(1, TILES - 1), middle[:])
             for b in range(first, last):
                 for n in range(NEIGHBOURS):
                     seen = sb([P, P], F32, "seen%d_%d_%d" % (TILES - 1, n, b))
                     look_up(TILES - 1, n, span(b), seen[:])
-                    add_turned(high[b - first][:, span(1)], seen[:], stop=(n == NEIGHBOURS - 1))
-            if last == BLOCKS:
-                w2_codes = sb([P, N], U32, "w2_codes", tag="w2_raw")
-                nc.vector.quantize_mx(out=w2_codes[:].bitcast(FP8X4), scales=w2_scale[:], in_=w2_grouped[:])
-                rr_first = second_product(*GROUPS[0], grouped[0], HALVES)
-            for b in range(first, last):
-                rectify(b, 1, high[b - first][:])
+                    add_turned(sums[b - first][TILES - 1], seen[:], stop=(n == NEIGHBOURS - 1))
+            if first == LAST:
+                w2_codes = sb([P, N], U32, "w2_codes", tag="w2_raw1")
+                rr_first = second_product(*GROUPS[0], grouped[0], HALVES, with_weights=True)
+                rectify(LAST, range(TILES - 1, TILES), final[:])
+            else:
+                for b in range(first, last):
+                    rectify(b, range(EARLY, TILES), high[b - first][:])
             grouped.append(turn_back(first, last))
 
         state_first = sb([P, HALVES, 2 * P], F32, "state_first", tag="h_rows3")
         update(*GROUPS[0], rr_first, 0, state=state_first[:, 0:1, :])
-        rr_second = second_product(*GROUPS[1], grouped[1], 1, chain)
+        rr_second = second_product(*GROUPS[1], grouped[1], 1, chain2)
         update(*GROUPS[0], rr_first, 1, moved_tag="h_grouped%d" % GROUPS[1][0], state=state_first[:, 1:2, :])
         rr_last = second_product(*GROUPS[2], grouped[2], HALVES)
         update(*GROUPS[1], rr_second, 0, moved_tag="h_grouped%d" % GROUPS[2][0])

@@ -71,8 +71,7 @@ def tile_picked_ynca_tanh_p_kernel(
         nc.scalar.activation(warm_out[:], warm[:], ACT.Tanh)
 
         w1_rows = w1.rearrange("(p t) c -> p t c", t=PACK)
-        w1_raw = [sb([P, PACK, P], F32, "w1_raw%d" % t) for t in range(EARLY)]
-        w1_rest = sb([P, PACK, (TILES - EARLY) * P], F32, "w1_rest")
+        w1_raw = [sb([P, PACK, P], F32, "w1_raw%d" % t) for t in range(TILES)]
         word_table = sb([P, T], U32, "word_table")
         kern_sb = [sb([P, S], F32, "kern%d" % n) for n in range(NEIGHBOURS)]
         pos_sb = [keep.tile([P, S // PER_COL], U16, name="pos%d" % n) for n in range(NEIGHBOURS)]
@@ -91,7 +90,8 @@ def tile_picked_ynca_tanh_p_kernel(
         for n, pos in enumerate((pos1, pos2)):
             nc.sync.dma_start(pos_sb[n][:], pos)
             nc.sync.dma_start(kern_sb[n][:], kern[n])
-        nc.sync.dma_start(w1_rest[:], w1_rows[:, :, span(EARLY, TILES)])
+        for t in range(EARLY, TILES):
+            nc.sync.dma_start(w1_raw[t][:], w1_rows[:, :, span(t)])
         for m in range(HALVES):
             nc.sync.dma_start(w2_raw[m][:], w2.rearrange("(p t) c -> p t c", t=PACK)[:, :, span(m)])
         nc.sync.dma_start(fire_rows[:], fire[0 : P // BLOCKS, :].rearrange("r (b j) -> (r b) j", j=P))
@@ -103,13 +103,12 @@ def tile_picked_ynca_tanh_p_kernel(
         x_scale = sb([P, S], U8, "x_scale")
         nc.vector.tensor_copy(x_scale[:], scale_table[:].indirect(offs_sb[:]))
 
-        w1_views = [raw[:] for raw in w1_raw] + [w1_rest[:, :, span(t)] for t in range(TILES - EARLY)]
         w1_codes = [sb([P, P], U32, "w1_codes%d" % t) for t in range(TILES)]
         w1_scale = [sb([P, P], U8, "w1_scale%d" % t) for t in range(TILES)]
 
         def quantise_w1(t, copy):
             grouped = sb([P, P * PACK], BF16, "w1_grouped%d" % t)
-            interleave(copy, grouped[:], w1_views[t])
+            interleave(copy, grouped[:], w1_raw[t][:])
             nc.vector.quantize_mx(out=w1_codes[t][:].bitcast(FP8X4), scales=w1_scale[t][:], in_=grouped[:])
 
         x_codes = sb([P, S], U32, "x_codes")
@@ -147,8 +146,7 @@ def tile_picked_ynca_tanh_p_kernel(
             quantise_w1(t, copy)
             acc = first_product(t, all_cells, "y_acc%d" % t)
             if t == EARLY:
-                for m in range(HALVES):
-                    interleave(nc.scalar.copy, w2_grouped[:, span(PACK * m, PACK * (m + 1))], w2_raw[m][:])
+                interleave(nc.scalar.copy, w2_grouped[:, span(0, PACK)], w2_raw[0][:])
                 y.append(sb([P, S], F32, "y%d" % t, tag="w2_raw0"))
             nc.scalar.copy(y[t][:, all_cells], acc[:])
 
@@ -156,6 +154,7 @@ def tile_picked_ynca_tanh_p_kernel(
             t = TILES - 1
             quantise_w1(t, nc.scalar.copy)
             acc = first_product(t, all_cells, "y_acc%d" % t, chain)
+            interleave(nc.scalar.copy, w2_grouped[:, span(PACK, 2 * PACK)], w2_raw[1][:])
             y.append(sb([P, S], F32, "y%d" % t, tag="w2_raw1"))
             nc.scalar.copy(y[t][:], acc[:])
 
@@ -234,7 +233,7 @@ def tile_picked_ynca_tanh_p_kernel(
 
         low = [bank([P, 2, EARLY * P], "pre_low%d" % i) for i in range(BLOCKS // 2)]
         make_y(1, nc.vector.tensor_copy)
-        slots = (("w1_grouped1", None), ("w1_grouped2", "w1_grouped3"))
+        slots = (("w1_raw1", None), ("w1_raw2", "w1_raw3"))
         for t in range(EARLY):
             for b in range(BLOCKS - t):
                 add_turned(low[b // 2][:, b % 2, span(t)], y[t][:, span(b)], start=(t == 0 and b % 2 == 0))
@@ -280,8 +279,7 @@ def tile_picked_ynca_tanh_p_kernel(
                     if first > 0:
                         seen = held[:, NEIGHBOURS * (t if first == LAST else 0) + n, :]
                     else:
-                        tag = "w1_codes%d" % (TILES - 1) if n == 0 else None
-                        seen = sb([P, cols.stop - cols.start], F32, "seen%d_%d_%d" % (t, n, first), tag=tag)[:]
+                        seen = sb([P, cols.stop - cols.start], F32, "seen%d_%d_%d" % (t, n, first))[:]
                     look_up(t, n, cols, seen)
                     for b in range(first, last):
                         closing = (b, t, n) == (LAST, TILES - 2, NEIGHBOURS - 1)

@@ -63,12 +63,8 @@ def tile_picked_ynca_tanh_p_kernel(
 
         scale_table = sb([P, T], U8, "scale_table")
         nc.vector.memset(scale_table[:].bitcast(I32), 0)
-        warm = sb([P, 1], F32, "warm")
-        warm_out = sb([P, 1], F32, "warm_out")
-        nc.vector.memset(warm[:], 0.0)
 
         offs_sb = keep.tile([P, S // PER_COL], U16, name="offs_sb")
-        nc.scalar.activation(warm_out[:], warm[:], ACT.Tanh)
 
         w1_rows = w1.rearrange("(p t) c -> p t c", t=PACK)
         w1_raw = [sb([P, PACK, P], F32, "w1_raw%d" % t) for t in range(TILES)]
@@ -103,13 +99,19 @@ def tile_picked_ynca_tanh_p_kernel(
         x_scale = sb([P, S], U8, "x_scale")
         nc.vector.tensor_copy(x_scale[:], scale_table[:].indirect(offs_sb[:]))
 
-        w1_codes = [sb([P, P], U32, "w1_codes%d" % t) for t in range(TILES)]
-        w1_scale = [sb([P, P], U8, "w1_scale%d" % t) for t in range(TILES)]
+        w1_codes = []
+        w1_scale = []
 
-        def quantise_w1(t, copy):
-            grouped = sb([P, P * PACK], BF16, "w1_grouped%d" % t)
-            interleave(copy, grouped[:], w1_raw[t][:])
-            nc.vector.quantize_mx(out=w1_codes[t][:].bitcast(FP8X4), scales=w1_scale[t][:], in_=grouped[:])
+        def quantise_w1(tiles, copy):
+            width = len(tiles) * P
+            grouped = sb([P, width * PACK], BF16, "w1_grouped%d" % tiles.start)
+            codes = sb([P, width], U32, "w1_codes%d" % tiles.start)
+            scale = sb([P, width], U8, "w1_scale%d" % tiles.start)
+            for i, t in enumerate(tiles):
+                interleave(copy, grouped[:, span(PACK * i, PACK * (i + 1))], w1_raw[t][:])
+                w1_codes.append(codes[:, span(i)])
+                w1_scale.append(scale[:, span(i)])
+            nc.vector.quantize_mx(out=codes[:].bitcast(FP8X4), scales=scale[:], in_=grouped[:])
 
         x_codes = sb([P, S], U32, "x_codes")
         y = [sb([P, S + SPARE if t == 0 else S], F32, "y%d" % t) for t in range(EARLY)]
@@ -119,8 +121,8 @@ def tile_picked_ynca_tanh_p_kernel(
             acc = bank([P, cols.stop - cols.start], name, pool)
             nc.tensor.matmul_mx(
                 out=acc[:],
-                lhsT=w1_codes[t][:].bitcast(FP8X4),
-                lhsT_scale=w1_scale[t][:],
+                lhsT=w1_codes[t].bitcast(FP8X4),
+                lhsT_scale=w1_scale[t],
                 rhs=x_codes[:, cols].bitcast(FP8X4),
                 rhs_scale=x_scale[:, cols],
                 start=True,
@@ -128,7 +130,7 @@ def tile_picked_ynca_tanh_p_kernel(
             )
             return acc
 
-        quantise_w1(0, nc.scalar.copy)
+        quantise_w1(range(0, 1), nc.scalar.copy)
         cell_halves = (span(0, BLOCKS // 2), span(BLOCKS // 2, BLOCKS))
         for cols in cell_halves:
             nc.vector.tensor_copy(x_codes[:, cols], word_table[:].indirect(entries(offs_sb, cols)))
@@ -142,21 +144,13 @@ def tile_picked_ynca_tanh_p_kernel(
         h_rows = [sb([P, H], BF16, "h_rows%d" % b) for b in range(BLOCKS)]
         all_cells = span(0, BLOCKS)
 
-        def make_y(t, copy):
-            quantise_w1(t, copy)
-            acc = first_product(t, all_cells, "y_acc%d" % t)
-            if t == EARLY:
-                interleave(nc.scalar.copy, w2_grouped[:, span(0, PACK)], w2_raw[0][:])
-                y.append(sb([P, S], F32, "y%d" % t, tag="w2_raw0"))
-            nc.scalar.copy(y[t][:, all_cells], acc[:])
-
-        def make_last_y():
-            t = TILES - 1
-            quantise_w1(t, nc.scalar.copy)
-            acc = first_product(t, all_cells, "y_acc%d" % t, chain)
-            interleave(nc.scalar.copy, w2_grouped[:, span(PACK, 2 * PACK)], w2_raw[1][:])
-            y.append(sb([P, S], F32, "y%d" % t, tag="w2_raw1"))
-            nc.scalar.copy(y[t][:], acc[:])
+        def make_late_tiles():
+            quantise_w1(range(EARLY, TILES), nc.scalar.copy)
+            accs = [first_product(t, all_cells, "y_acc%d" % t, pool) for t, pool in ((EARLY, ring), (EARLY + 1, chain))]
+            for m, acc in enumerate(accs):
+                interleave(nc.scalar.copy, w2_grouped[:, span(PACK * m, PACK * (m + 1))], w2_raw[m][:])
+                y.append(sb([P, S], F32, "y%d" % (EARLY + m), tag="w2_raw%d" % m))
+                nc.scalar.copy(y[EARLY + m][:], acc[:])
 
         def look_up(t, n, cols, seen):
             nc.vector.tensor_tensor(seen, y[t][:].indirect(entries(pos_sb[n], cols)), kern_sb[n][:, cols], ALU.mult)
@@ -232,19 +226,19 @@ def tile_picked_ynca_tanh_p_kernel(
             nc.sync.dma_start(out_rows[:, rows, cols], state)
 
         low = [bank([P, 2, EARLY * P], "pre_low%d" % i) for i in range(BLOCKS // 2)]
-        make_y(1, nc.vector.tensor_copy)
-        slots = (("w1_raw1", None), ("w1_raw2", "w1_raw3"))
+        quantise_w1(range(1, 2), nc.vector.tensor_copy)
+        nc.scalar.copy(y[1][:], first_product(1, all_cells, "y_acc1")[:])
         for t in range(EARLY):
             for b in range(BLOCKS - t):
                 add_turned(low[b // 2][:, b % 2, span(t)], y[t][:, span(b)], start=(t == 0 and b % 2 == 0))
         for t in range(EARLY):
-            if t == EARLY - 1:
-                make_y(EARLY, nc.scalar.copy)
-                make_last_y()
             blocks = BLOCKS - t
+            if t == EARLY - 1:
+                make_late_tiles()
+                pair = sb([P, NEIGHBOURS, (BLOCKS - 1) * P], F32, "seen1", tag="w1_raw3")
             for n in range(NEIGHBOURS):
-                seen = sb([P, blocks * P], F32, "seen%d_%d" % (t, n), tag=slots[t][n])
-                look_up(t, n, span(0, blocks), seen[:])
+                seen = pair[:, n, :] if t else sb([P, S], F32, "seen0_%d" % n, tag=None if n else "w1_raw1")[:]
+                look_up(t, n, span(0, blocks), seen)
                 for b in range(blocks):
                     closing = t == EARLY - 1 and n == NEIGHBOURS - 1 and b > 0
                     add_turned(low[b // 2][:, b % 2, span(t)], seen[:, span(b)], stop=closing)

@@ -24,7 +24,6 @@ NEIGHBOURS = 2
 TILES = H // P
 BLOCKS = S // P
 HALVES = N // P
-BANKS = 8
 EARLY = 2
 SPARE = 16
 GROUPS = ((0, 2), (2, 3), (3, 4))
@@ -51,15 +50,13 @@ def tile_picked_ynca_tanh_p_kernel(
     nc = tc.nc
     with ExitStack() as ctx:
         keep = ctx.enter_context(tc.tile_pool(name="keep", bufs=1))
-        ring = ctx.enter_context(tc.psum_pool(name="ring", bufs=BANKS - 2))
-        chain = ctx.enter_context(tc.psum_pool(name="chain", bufs=1))
-        chain2 = ctx.enter_context(tc.psum_pool(name="chain2", bufs=1))
+        banks = ctx.enter_context(tc.psum_pool(name="banks", bufs=1))
 
         def sb(shape, dtype, name, tag=None):
             return keep.tile(shape, dtype, name=name, tag=tag or name, align_bytes=64)
 
-        def bank(shape, name, pool=ring):
-            return pool.tile(shape, F32, name=name, tag="bank")
+        def bank(shape, name, number):
+            return banks.tile(shape, F32, name=name, tag="bank%d" % number)
 
         scale_table = sb([P, T], U8, "scale_table")
         nc.vector.memset(scale_table[:].bitcast(I32), 0)
@@ -117,8 +114,8 @@ def tile_picked_ynca_tanh_p_kernel(
         y = [sb([P, S + SPARE if t == 0 else S], F32, "y%d" % t) for t in range(EARLY)]
         nc.gpsimd.memset(y[0][:, S:], 0.0)
 
-        def first_product(t, cols, name, pool=ring):
-            acc = bank([P, cols.stop - cols.start], name, pool)
+        def first_product(t, cols, name, number):
+            acc = bank([P, cols.stop - cols.start], name, number)
             nc.tensor.matmul_mx(
                 out=acc[:],
                 lhsT=w1_codes[t].bitcast(FP8X4),
@@ -134,10 +131,11 @@ def tile_picked_ynca_tanh_p_kernel(
         cell_halves = (span(0, BLOCKS // 2), span(BLOCKS // 2, BLOCKS))
         for cols in cell_halves:
             nc.vector.tensor_copy(x_codes[:, cols], word_table[:].indirect(entries(offs_sb, cols)))
-        for cols in [cell_halves[0]] + [span(b) for b in range(BLOCKS // 2, BLOCKS)]:
-            acc = first_product(0, cols, "y_acc0_%d" % cols.start)
+        for i, cols in enumerate([cell_halves[0]] + [span(b) for b in range(BLOCKS // 2, BLOCKS)]):
+            acc = first_product(0, cols, "y_acc0_%d" % cols.start, i)
             nc.scalar.copy(y[0][:, cols], acc[:])
 
+        chain, chain2 = 6, 7
         fire_col = sb([P, BLOCKS], F32, "fire_col")
         w2_scale = sb([P, N], U8, "w2_scale")
         w2_grouped = sb([P, N * PACK], BF16, "w2_grouped")
@@ -146,7 +144,7 @@ def tile_picked_ynca_tanh_p_kernel(
 
         def make_late_tiles():
             quantise_w1(range(EARLY, TILES), nc.scalar.copy)
-            accs = [first_product(t, all_cells, "y_acc%d" % t, pool) for t, pool in ((EARLY, ring), (EARLY + 1, chain))]
+            accs = [first_product(t, all_cells, "y_acc%d" % t, pool) for t, pool in ((EARLY, 0), (EARLY + 1, chain))]
             for m, acc in enumerate(accs):
                 interleave(nc.scalar.copy, w2_grouped[:, span(PACK * m, PACK * (m + 1))], w2_raw[m][:])
                 y.append(sb([P, S], F32, "y%d" % (EARLY + m), tag="w2_raw%d" % m))
@@ -171,7 +169,7 @@ def tile_picked_ynca_tanh_p_kernel(
             grouped = sb([P, (last - first) * P * PACK], BF16, "h_grouped%d" % first)
             words = grouped[:].bitcast(F32)
             for b in range(first, last):
-                turned = bank([P, 2, P], "h_turned%d" % b, chain if b == 0 else ring)
+                turned = bank([P, 2, P], "h_turned%d" % b, (chain, 3, 4, 1)[b])
                 pairs = h_rows[b][:].bitcast(F32)
                 for u in range(2):
                     nc.tensor.transpose(turned[:, u, :], pairs[:, span(u)], ident[:])
@@ -188,7 +186,7 @@ def tile_picked_ynca_tanh_p_kernel(
                 in_=w2_grouped[:, span(PACK * m, PACK * (m + 1))],
             )
 
-        def second_product(first, last, grouped, parts, pool=ring, with_weights=False):
+        def second_product(first, last, grouped, numbers, with_weights=False):
             width = (last - first) * P
             h_codes = sb([P, width], U32, "h_codes%d" % first)
             h_scale = sb([P, width], U8, "h_scale%d" % first)
@@ -197,8 +195,8 @@ def tile_picked_ynca_tanh_p_kernel(
             nc.vector.quantize_mx(out=h_codes[:].bitcast(FP8X4), scales=h_scale[:], in_=grouped[:])
             if with_weights:
                 quantise_w2(1)
-            per = HALVES // parts
-            rr = [bank([P, per, width], "rr%d_%d" % (first, i), pool) for i in range(parts)]
+            per = HALVES // len(numbers)
+            rr = [bank([P, per, width], "rr%d_%d" % (first, i), number) for i, number in enumerate(numbers)]
             for m in range(HALVES):
                 nc.tensor.matmul_mx(
                     out=rr[m // per][:, m % per, :],
@@ -225,12 +223,12 @@ def tile_picked_ynca_tanh_p_kernel(
             nc.scalar.activation(state, moved[:], ACT.Tanh)
             nc.sync.dma_start(out_rows[:, rows, cols], state)
 
-        low = [bank([P, 2, EARLY * P], "pre_low%d" % i) for i in range(BLOCKS // 2)]
+        low = [bank([P, 2, EARLY * P], "pre_low%d" % i, 3 + i) for i in range(BLOCKS // 2)]
         quantise_w1(range(1, 2), nc.vector.tensor_copy)
-        nc.scalar.copy(y[1][:], first_product(1, all_cells, "y_acc1")[:])
-        for t in range(EARLY):
+        nc.scalar.copy(y[1][:], first_product(1, all_cells, "y_acc1", 5)[:])
+        for t in reversed(range(EARLY)):
             for b in range(BLOCKS - t):
-                add_turned(low[b // 2][:, b % 2, span(t)], y[t][:, span(b)], start=(t == 0 and b % 2 == 0))
+                add_turned(low[b // 2][:, b % 2, span(t)], y[t][:, span(b)], start=(t == EARLY - 1 and b % 2 == 0))
         for t in range(EARLY):
             blocks = BLOCKS - t
             if t == EARLY - 1:
@@ -250,6 +248,9 @@ def tile_picked_ynca_tanh_p_kernel(
             tiles = 1 if b == BLOCKS - 1 else EARLY
             rectify(b, range(tiles), low[b // 2][:, b % 2, span(0, tiles)])
 
+        def warm_up(number):
+            first_product(0, cell_halves[0], "warm_up%d" % number, number)
+
         grouped = []
         LAST = BLOCKS - 1
         for first, last in GROUPS:
@@ -260,7 +261,7 @@ def tile_picked_ynca_tanh_p_kernel(
                 final = bank([P, P], "pre_final", chain2)
                 sums = [{1: middle[:, span(0)], 2: middle[:, span(1)], 3: final[:]}]
             else:
-                high = [bank([P, 2 * P], "pre_high%d" % b, chain2 if first else ring) for b in range(first, last)]
+                high = [bank([P, 2 * P], "pre_high%d" % b, (1, 2, chain2)[b]) for b in range(first, last)]
                 sums = [{t: acc[:, span(t - EARLY)] for t in tiles} for acc in high]
             for t in tiles:
                 for b in range(first, last):
@@ -279,6 +280,7 @@ def tile_picked_ynca_tanh_p_kernel(
                         closing = (b, t, n) == (LAST, TILES - 2, NEIGHBOURS - 1)
                         add_turned(sums[b - first][t], seen[:, span(b - first)], stop=closing)
             if first == LAST:
+                warm_up(2)
                 rectify(LAST, range(1, TILES - 1), middle[:])
             for b in range(first, last):
                 for n in range(NEIGHBOURS):
@@ -287,18 +289,19 @@ def tile_picked_ynca_tanh_p_kernel(
                     add_turned(sums[b - first][TILES - 1], seen[:], stop=(n == NEIGHBOURS - 1))
             if first == LAST:
                 w2_codes = sb([P, N], U32, "w2_codes", tag="w2_raw1")
-                rr_first = second_product(*GROUPS[0], grouped[0], HALVES, with_weights=True)
+                rr_first = second_product(*GROUPS[0], grouped[0], (5, 0), with_weights=True)
                 rectify(LAST, range(TILES - 1, TILES), final[:])
             else:
+                warm_up(1 if first else 4)
                 for b in range(first, last):
                     rectify(b, range(EARLY, TILES), high[b - first][:])
             grouped.append(turn_back(first, last))
 
         state_first = sb([P, HALVES, 2 * P], F32, "state_first", tag="h_rows3")
         update(*GROUPS[0], rr_first, 0, state=state_first[:, 0:1, :])
-        rr_second = second_product(*GROUPS[1], grouped[1], 1, chain2)
+        rr_second = second_product(*GROUPS[1], grouped[1], (chain2,))
         update(*GROUPS[0], rr_first, 1, moved_tag="h_grouped%d" % GROUPS[1][0], state=state_first[:, 1:2, :])
-        rr_last = second_product(*GROUPS[2], grouped[2], HALVES)
+        rr_last = second_product(*GROUPS[2], grouped[2], (2, 3))
         update(*GROUPS[1], rr_second, 0, moved_tag="h_grouped%d" % GROUPS[2][0])
         for i in range(HALVES):
             update(*GROUPS[2], rr_last, i)

@@ -134,6 +134,8 @@ def tile_picked_ynca_tanh_p_kernel(
         for i, cols in enumerate([cell_halves[0]] + [span(b) for b in range(BLOCKS // 2, BLOCKS)]):
             acc = first_product(0, cols, "y_acc0_%d" % cols.start, i)
             nc.scalar.copy(y[0][:, cols], acc[:])
+            if i == 0:
+                first_product(0, cols, "warm_up0", 7)
 
         chain, chain2 = 6, 7
         fire_col = sb([P, BLOCKS], F32, "fire_col")
@@ -226,6 +228,7 @@ def tile_picked_ynca_tanh_p_kernel(
         low = [bank([P, 2, EARLY * P], "pre_low%d" % i, 3 + i) for i in range(BLOCKS // 2)]
         quantise_w1(range(1, 2), nc.vector.tensor_copy)
         nc.scalar.copy(y[1][:], first_product(1, all_cells, "y_acc1", 5)[:])
+        first_product(1, all_cells, "warm_up1", 6)
         for t in reversed(range(EARLY)):
             for b in range(BLOCKS - t):
                 add_turned(low[b // 2][:, b % 2, span(t)], y[t][:, span(b)], start=(t == EARLY - 1 and b % 2 == 0))
@@ -247,9 +250,6 @@ def tile_picked_ynca_tanh_p_kernel(
         for b in range(BLOCKS):
             tiles = 1 if b == BLOCKS - 1 else EARLY
             rectify(b, range(tiles), low[b // 2][:, b % 2, span(0, tiles)])
-
-        def warm_up(number):
-            first_product(0, cell_halves[0], "warm_up%d" % number, number)
 
         grouped = []
         LAST = BLOCKS - 1
@@ -280,7 +280,6 @@ def tile_picked_ynca_tanh_p_kernel(
                         closing = (b, t, n) == (LAST, TILES - 2, NEIGHBOURS - 1)
                         add_turned(sums[b - first][t], seen[:, span(b - first)], stop=closing)
             if first == LAST:
-                warm_up(2)
                 rectify(LAST, range(1, TILES - 1), middle[:])
             for b in range(first, last):
                 for n in range(NEIGHBOURS):
@@ -292,7 +291,6 @@ def tile_picked_ynca_tanh_p_kernel(
                 rr_first = second_product(*GROUPS[0], grouped[0], (5, 0), with_weights=True)
                 rectify(LAST, range(TILES - 1, TILES), final[:])
             else:
-                warm_up(1 if first else 4)
                 for b in range(first, last):
                     rectify(b, range(EARLY, TILES), high[b - first][:])
             grouped.append(turn_back(first, last))

@@ -147,6 +147,7 @@ def tile_picked_ynca_tanh_p_kernel(
         def make_late_tiles():
             quantise_w1(range(EARLY, TILES), nc.scalar.copy)
             accs = [first_product(t, all_cells, "y_acc%d" % t, pool) for t, pool in ((EARLY, 0), (EARLY + 1, chain))]
+            first_product(EARLY + 1, all_cells, "warm_up1", 5)
             for m, acc in enumerate(accs):
                 interleave(nc.scalar.copy, w2_grouped[:, span(PACK * m, PACK * (m + 1))], w2_raw[m][:])
                 y.append(sb([P, S], F32, "y%d" % (EARLY + m), tag="w2_raw%d" % m))
@@ -225,13 +226,13 @@ def tile_picked_ynca_tanh_p_kernel(
             nc.scalar.activation(state, moved[:], ACT.Tanh)
             nc.sync.dma_start(out_rows[:, rows, cols], state)
 
-        low = [bank([P, 2, EARLY * P], "pre_low%d" % i, 3 + i) for i in range(BLOCKS // 2)]
         quantise_w1(range(1, 2), nc.vector.tensor_copy)
-        nc.scalar.copy(y[1][:], first_product(1, all_cells, "y_acc1", 5)[:])
-        first_product(1, all_cells, "warm_up1", 6)
-        for t in reversed(range(EARLY)):
+        for i, cols in enumerate(cell_halves):
+            nc.scalar.copy(y[1][:, cols], first_product(1, cols, "y_acc1_%d" % i, 4 + i)[:])
+        low = [bank([P, 2, EARLY * P], "pre_low%d" % i, 3 + i) for i in range(BLOCKS // 2)]
+        for t in range(EARLY):
             for b in range(BLOCKS - t):
-                add_turned(low[b // 2][:, b % 2, span(t)], y[t][:, span(b)], start=(t == EARLY - 1 and b % 2 == 0))
+                add_turned(low[b // 2][:, b % 2, span(t)], y[t][:, span(b)], start=(t == 0 and b % 2 == 0))
         for t in range(EARLY):
             blocks = BLOCKS - t
             if t == EARLY - 1:

@@ -24,8 +24,13 @@ NEIGHBOURS = 2
 TILES = H // P
 BLOCKS = S // P
 HALVES = N // P
+SCALE_ROWS = 4
+LAST_TILE = TILES - 1
+LAST_BLOCK = BLOCKS - 1
 EARLY = 2
 SPARE = 16
+AHEAD = T // 4
+ROW_BYTES = 4 * S
 GROUPS = ((0, 2), (2, 3), (3, 4))
 
 
@@ -51,6 +56,8 @@ def tile_picked_ynca_tanh_p_kernel(
     with ExitStack() as ctx:
         keep = ctx.enter_context(tc.tile_pool(name="keep", bufs=1))
         banks = ctx.enter_context(tc.psum_pool(name="banks", bufs=1))
+        placed = ctx.enter_context(tc.tile_pool(name="placed", bufs=1))
+        raw_at = 4 * ROW_BYTES
 
         def sb(shape, dtype, name, tag=None):
             return keep.tile(shape, dtype, name=name, tag=tag or name, align_bytes=64)
@@ -64,7 +71,10 @@ def tile_picked_ynca_tanh_p_kernel(
         offs_sb = keep.tile([P, S // PER_COL], U16, name="offs_sb")
 
         w1_rows = w1.rearrange("(p t) c -> p t c", t=PACK)
-        w1_raw = [sb([P, PACK, P], F32, "w1_raw%d" % t) for t in range(TILES)]
+        w1_first = sb([P, PACK, P], F32, "w1_first")
+        w1_middle = sb([P, PACK, 2 * P], F32, "w1_middle")
+        w1_last = placed.tile([P, PACK, P], F32, name="w1_last", align_bytes=64, offset=raw_at)
+        w1_raw = [w1_first[:], w1_middle[:, :, span(0)], w1_middle[:, :, span(1)], w1_last[:]]
         word_table = sb([P, T], U32, "word_table")
         kern_sb = [sb([P, S], F32, "kern%d" % n) for n in range(NEIGHBOURS)]
         pos_sb = [keep.tile([P, S // PER_COL], U16, name="pos%d" % n) for n in range(NEIGHBOURS)]
@@ -72,19 +82,18 @@ def tile_picked_ynca_tanh_p_kernel(
         fire_rows = sb([P, P], F32, "fire_rows")
         cur_sb = sb([P, HALVES, S], F32, "cur_sb")
 
-        nc.sync.dma_start(w1_raw[0][:], w1_rows[:, :, span(0)])
+        nc.sync.dma_start(w1_first[:], w1_rows[:, :, span(0)])
         nc.sync.dma_start(offs_sb[:], offs)
         word_rows = x_words[0].rearrange("p n t -> p (n t)").bitcast(I32)
-        nc.sync.dma_start(word_table[:, : T // 4].bitcast(I32), word_rows[:, : T // 4])
-        for r in range(4):
-            nc.sync.dma_start(scale_table[r:P:QUADRANT, :].bitcast(I32), x_scales[0, r::4, :].bitcast(I32))
-        nc.sync.dma_start(word_table[:, T // 4 :].bitcast(I32), word_rows[:, T // 4 :])
-        nc.sync.dma_start(w1_raw[1][:], w1_rows[:, :, span(1)])
+        nc.sync.dma_start(word_table[:, :AHEAD].bitcast(I32), word_rows[:, :AHEAD])
+        for r in range(SCALE_ROWS):
+            nc.sync.dma_start(scale_table[r:P:QUADRANT, :].bitcast(I32), x_scales[0, r::SCALE_ROWS, :].bitcast(I32))
+        nc.sync.dma_start(word_table[:, AHEAD:].bitcast(I32), word_rows[:, AHEAD:])
+        nc.sync.dma_start(w1_middle[:], w1_rows[:, :, span(1, LAST_TILE)])
         for n, pos in enumerate((pos1, pos2)):
             nc.sync.dma_start(pos_sb[n][:], pos)
             nc.sync.dma_start(kern_sb[n][:], kern[n])
-        for t in range(EARLY, TILES):
-            nc.sync.dma_start(w1_raw[t][:], w1_rows[:, :, span(t)])
+        nc.sync.dma_start(w1_last[:], w1_rows[:, :, span(LAST_TILE)])
         for m in range(HALVES):
             nc.sync.dma_start(w2_raw[m][:], w2.rearrange("(p t) c -> p t c", t=PACK)[:, :, span(m)])
         nc.sync.dma_start(fire_rows[:], fire[0 : P // BLOCKS, :].rearrange("r (b j) -> (r b) j", j=P))
@@ -100,15 +109,15 @@ def tile_picked_ynca_tanh_p_kernel(
         w1_scale = []
 
         def quantise_w1(tiles, copy):
-            width = len(tiles) * P
-            grouped = sb([P, width * PACK], BF16, "w1_grouped%d" % tiles.start)
-            codes = sb([P, width], U32, "w1_codes%d" % tiles.start)
-            scale = sb([P, width], U8, "w1_scale%d" % tiles.start)
+            grouped = [sb([P, P * PACK], BF16, "w1_grouped%d" % t) for t in tiles]
             for i, t in enumerate(tiles):
-                interleave(copy, grouped[:, span(PACK * i, PACK * (i + 1))], w1_raw[t][:])
-                w1_codes.append(codes[:, span(i)])
-                w1_scale.append(scale[:, span(i)])
-            nc.vector.quantize_mx(out=codes[:].bitcast(FP8X4), scales=scale[:], in_=grouped[:])
+                interleave(copy, grouped[i][:], w1_raw[t])
+            for i, t in enumerate(tiles):
+                codes = sb([P, P], U32, "w1_codes%d" % t)
+                scale = sb([P, P], U8, "w1_scale%d" % t)
+                w1_codes.append(codes[:])
+                w1_scale.append(scale[:])
+                nc.vector.quantize_mx(out=codes[:].bitcast(FP8X4), scales=scale[:], in_=grouped[i][:])
 
         x_codes = sb([P, S], U32, "x_codes")
         y = [sb([P, S + SPARE if t == 0 else S], F32, "y%d" % t) for t in range(EARLY)]
@@ -137,21 +146,11 @@ def tile_picked_ynca_tanh_p_kernel(
             if i == 0:
                 first_product(0, cols, "warm_up0", 7)
 
-        chain, chain2 = 6, 7
         fire_col = sb([P, BLOCKS], F32, "fire_col")
         w2_scale = sb([P, N], U8, "w2_scale")
         w2_grouped = sb([P, N * PACK], BF16, "w2_grouped")
         h_rows = [sb([P, H], BF16, "h_rows%d" % b) for b in range(BLOCKS)]
         all_cells = span(0, BLOCKS)
-
-        def make_late_tiles():
-            quantise_w1(range(EARLY, TILES), nc.scalar.copy)
-            accs = [first_product(t, all_cells, "y_acc%d" % t, pool) for t, pool in ((EARLY, 0), (EARLY + 1, chain))]
-            first_product(EARLY + 1, all_cells, "warm_up1", 5)
-            for m, acc in enumerate(accs):
-                interleave(nc.scalar.copy, w2_grouped[:, span(PACK * m, PACK * (m + 1))], w2_raw[m][:])
-                y.append(sb([P, S], F32, "y%d" % (EARLY + m), tag="w2_raw%d" % m))
-                nc.scalar.copy(y[EARLY + m][:], acc[:])
 
         def look_up(t, n, cols, seen):
             nc.vector.tensor_tensor(seen, y[t][:].indirect(entries(pos_sb[n], cols)), kern_sb[n][:, cols], ALU.mult)
@@ -168,11 +167,11 @@ def tile_picked_ynca_tanh_p_kernel(
                 scale=fire_col[:, b : b + 1],
             )
 
-        def turn_back(first, last):
+        def turn_back(first, last, numbers):
             grouped = sb([P, (last - first) * P * PACK], BF16, "h_grouped%d" % first)
             words = grouped[:].bitcast(F32)
             for b in range(first, last):
-                turned = bank([P, 2, P], "h_turned%d" % b, (chain, 3, 4, 1)[b])
+                turned = bank([P, 2, P], "h_turned%d" % b, numbers[b - first])
                 pairs = h_rows[b][:].bitcast(F32)
                 for u in range(2):
                     nc.tensor.transpose(turned[:, u, :], pairs[:, span(u)], ident[:])
@@ -226,81 +225,115 @@ def tile_picked_ynca_tanh_p_kernel(
             nc.scalar.activation(state, moved[:], ACT.Tanh)
             nc.sync.dma_start(out_rows[:, rows, cols], state)
 
-        quantise_w1(range(1, 2), nc.vector.tensor_copy)
+        def own(target, t, b, start):
+            add_turned(target, y[t][:, span(b)], start=start)
+
+        def neighbours(target, t, b, seen, stop):
+            for n in range(NEIGHBOURS):
+                term = seen(n)
+                look_up(t, n, span(b), term)
+                add_turned(target, term, stop=(stop and n == NEIGHBOURS - 1))
+
+        def fresh(b):
+            return lambda n: sb([P, P], F32, "seen%d_%d_%d" % (LAST_TILE, n, b))[:]
+
+        quantise_w1(range(1, LAST_TILE), nc.vector.tensor_copy)
         for i, cols in enumerate(cell_halves):
             nc.scalar.copy(y[1][:, cols], first_product(1, cols, "y_acc1_%d" % i, 4 + i)[:])
+        y.append(placed.tile([P, S], F32, name="y2", align_bytes=64, offset=raw_at + ROW_BYTES // 2))
+        acc_two = first_product(2, all_cells, "y_acc2", 0)
+
         low = [bank([P, 2, EARLY * P], "pre_low%d" % i, 3 + i) for i in range(BLOCKS // 2)]
+
+        def early_sum(t, b):
+            return low[b // 2][:, b % 2, span(t)]
+
         for t in range(EARLY):
             for b in range(BLOCKS - t):
-                add_turned(low[b // 2][:, b % 2, span(t)], y[t][:, span(b)], start=(t == 0 and b % 2 == 0))
-        for t in range(EARLY):
-            blocks = BLOCKS - t
-            if t == EARLY - 1:
-                make_late_tiles()
-                pair = sb([P, NEIGHBOURS, (BLOCKS - 1) * P], F32, "seen1", tag="w1_raw3")
-            for n in range(NEIGHBOURS):
-                seen = pair[:, n, :] if t else sb([P, S], F32, "seen0_%d" % n, tag=None if n else "w1_raw1")[:]
-                look_up(t, n, span(0, blocks), seen)
-                for b in range(blocks):
-                    closing = t == EARLY - 1 and n == NEIGHBOURS - 1 and b > 0
-                    add_turned(low[b // 2][:, b % 2, span(t)], seen[:, span(b)], stop=closing)
+                own(early_sum(t, b), t, b, t == 0 and b % 2 == 0)
+        for n in range(NEIGHBOURS):
+            seen = sb([P, S], F32, "seen0_%d" % n, tag=None if n else "w1_middle")
+            look_up(0, n, all_cells, seen[:])
+            for b in range(BLOCKS):
+                add_turned(early_sum(0, b), seen[:, span(b)])
 
-        fire_turned = bank([P, P], "fire_turned", chain)
+        quantise_w1(range(LAST_TILE, TILES), nc.scalar.copy)
+        nc.scalar.copy(y[2][:], acc_two[:])
+        acc_last = first_product(LAST_TILE, all_cells, "y_acc3", 6)
+        first_product(LAST_TILE, all_cells, "warm_up1", 5)
+        for m in range(HALVES):
+            interleave(nc.scalar.copy, w2_grouped[:, span(PACK * m, PACK * (m + 1))], w2_raw[m][:])
+        y.append(sb([P, S], F32, "y3", tag="w2_raw1"))
+        nc.scalar.copy(y[LAST_TILE][:], acc_last[:])
+
+        pieces = LAST_BLOCK + 2
+        seen_middle = placed.tile(
+            [P, NEIGHBOURS, pieces * P],
+            F32,
+            name="seen1",
+            align_bytes=64,
+            offset=raw_at + ROW_BYTES // 4 - NEIGHBOURS * pieces * P * 4,
+        )
+        for n in range(NEIGHBOURS):
+            look_up(1, n, span(0, LAST_BLOCK), seen_middle[:, n, span(0, LAST_BLOCK)])
+            for b in range(LAST_BLOCK):
+                add_turned(early_sum(1, b), seen_middle[:, n, span(b)], stop=(n == NEIGHBOURS - 1 and b > 0))
+
+        fire_turned = bank([P, P], "fire_turned", 6)
         nc.tensor.transpose(fire_turned[:], fire_rows[:], ident[:])
         nc.scalar.copy(fire_col[:], fire_turned[:, 0:BLOCKS])
         for b in range(BLOCKS):
-            tiles = 1 if b == BLOCKS - 1 else EARLY
+            tiles = 1 if b == LAST_BLOCK else EARLY
             rectify(b, range(tiles), low[b // 2][:, b % 2, span(0, tiles)])
 
-        grouped = []
-        LAST = BLOCKS - 1
-        for first, last in GROUPS:
-            cols = span(first, last)
-            tiles = range(1 if first == LAST else EARLY, TILES)
-            if first == LAST:
-                middle = bank([P, 2 * P], "pre_middle", chain)
-                final = bank([P, P], "pre_final", chain2)
-                sums = [{1: middle[:, span(0)], 2: middle[:, span(1)], 3: final[:]}]
-            else:
-                high = [bank([P, 2 * P], "pre_high%d" % b, (1, 2, chain2)[b]) for b in range(first, last)]
-                sums = [{t: acc[:, span(t - EARLY)] for t in tiles} for acc in high]
-            for t in tiles:
-                for b in range(first, last):
-                    opening = t == tiles.start or (b, t) == (LAST, TILES - 1)
-                    add_turned(sums[b - first][t], y[t][:, span(b)], start=opening)
-            if first == GROUPS[1][0]:
-                held = sb([P, 3 * NEIGHBOURS, P], F32, "seen_held", tag="fire_rows")
-            for t in tiles[:-1]:
-                for n in range(NEIGHBOURS):
-                    if first > 0:
-                        seen = held[:, NEIGHBOURS * (t if first == LAST else 0) + n, :]
-                    else:
-                        seen = sb([P, cols.stop - cols.start], F32, "seen%d_%d_%d" % (t, n, first))[:]
-                    look_up(t, n, cols, seen)
-                    for b in range(first, last):
-                        closing = (b, t, n) == (LAST, TILES - 2, NEIGHBOURS - 1)
-                        add_turned(sums[b - first][t], seen[:, span(b - first)], stop=closing)
-            if first == LAST:
-                rectify(LAST, range(1, TILES - 1), middle[:])
-            for b in range(first, last):
-                for n in range(NEIGHBOURS):
-                    seen = sb([P, P], F32, "seen%d_%d_%d" % (TILES - 1, n, b))
-                    look_up(TILES - 1, n, span(b), seen[:])
-                    add_turned(sums[b - first][TILES - 1], seen[:], stop=(n == NEIGHBOURS - 1))
-            if first == LAST:
-                w2_codes = sb([P, N], U32, "w2_codes", tag="w2_raw1")
-                rr_first = second_product(*GROUPS[0], grouped[0], (5, 0), with_weights=True)
-                rectify(LAST, range(TILES - 1, TILES), final[:])
-            else:
-                for b in range(first, last):
-                    rectify(b, range(EARLY, TILES), high[b - first][:])
-            grouped.append(turn_back(first, last))
+        high = [bank([P, 2 * P], "pre_high%d" % b, 1 + b) for b in range(2)]
+        for t in range(EARLY, TILES):
+            for b in range(2):
+                own(high[b][:, span(t - EARLY)], t, b, t == EARLY)
+        for n in range(NEIGHBOURS):
+            seen = seen_middle[:, n, span(LAST_BLOCK, pieces)]
+            look_up(2, n, span(0, 2), seen)
+            for b in range(2):
+                add_turned(high[b][:, span(0)], seen[:, span(b)])
+        for b in range(2):
+            neighbours(high[b][:, span(1)], LAST_TILE, b, fresh(b), True)
+        for b in range(2):
+            rectify(b, range(EARLY, TILES), high[b][:])
+        grouped_first = turn_back(*GROUPS[0], (6, 3))
 
-        state_first = sb([P, HALVES, 2 * P], F32, "state_first", tag="h_rows3")
+        second = [bank([P, P], "pre_second%d" % t, number) for t, number in ((2, 7), (LAST_TILE, 2))]
+        for i, acc in enumerate(second):
+            own(acc[:], EARLY + i, 2, True)
+        held = sb([P, 3 * NEIGHBOURS, P], F32, "seen_held", tag="fire_rows")
+
+        def held_piece(i):
+            return lambda n: held[:, NEIGHBOURS * i + n, :]
+
+        neighbours(second[0][:], 2, 2, held_piece(0), True)
+        rectify(2, range(2, LAST_TILE), second[0][:])
+        neighbours(second[1][:], LAST_TILE, 2, fresh(2), True)
+        rectify(2, range(LAST_TILE, TILES), second[1][:])
+        grouped_second = turn_back(*GROUPS[1], (4,))
+
+        middle = bank([P, 2 * P], "pre_middle", 6)
+        final = bank([P, P], "pre_final", 2)
+        for t in range(1, LAST_TILE):
+            own(middle[:, span(t - 1)], t, LAST_BLOCK, t == 1)
+        own(final[:], LAST_TILE, LAST_BLOCK, True)
+        for t in range(1, LAST_TILE):
+            neighbours(middle[:, span(t - 1)], t, LAST_BLOCK, held_piece(t), t == LAST_TILE - 1)
+        rectify(LAST_BLOCK, range(1, LAST_TILE), middle[:])
+        neighbours(final[:], LAST_TILE, LAST_BLOCK, fresh(LAST_BLOCK), True)
+        w2_codes = sb([P, N], U32, "w2_codes", tag="w2_raw1")
+        rr_first = second_product(*GROUPS[0], grouped_first, (5, 0), with_weights=True)
+        rectify(LAST_BLOCK, range(LAST_TILE, TILES), final[:])
+        grouped_last = turn_back(*GROUPS[2], (1,))
+
+        state_first = sb([P, HALVES, 2 * P], F32, "state_first", tag="h_rows%d" % LAST_BLOCK)
         update(*GROUPS[0], rr_first, 0, state=state_first[:, 0:1, :])
-        rr_second = second_product(*GROUPS[1], grouped[1], (chain2,))
+        rr_second = second_product(*GROUPS[1], grouped_second, (2,))
         update(*GROUPS[0], rr_first, 1, moved_tag="h_grouped%d" % GROUPS[1][0], state=state_first[:, 1:2, :])
-        rr_last = second_product(*GROUPS[2], grouped[2], (2, 3))
+        rr_last = second_product(*GROUPS[2], grouped_last, (7, 3))
         update(*GROUPS[1], rr_second, 0, moved_tag="h_grouped%d" % GROUPS[2][0])
         for i in range(HALVES):
             update(*GROUPS[2], rr_last, i)

@@ -143,8 +143,6 @@ def tile_picked_ynca_tanh_p_kernel(
         for i, cols in enumerate([cell_halves[0]] + [span(b) for b in range(BLOCKS // 2, BLOCKS)]):
             acc = first_product(0, cols, "y_acc0_%d" % cols.start, i)
             nc.scalar.copy(y[0][:, cols], acc[:])
-            if i == 0:
-                first_product(0, cols, "warm_up0", 7)
 
         fire_col = sb([P, BLOCKS], F32, "fire_col")
         w2_scale = sb([P, N], U8, "w2_scale")
@@ -260,7 +258,6 @@ def tile_picked_ynca_tanh_p_kernel(
         quantise_w1(range(LAST_TILE, TILES), nc.scalar.copy)
         nc.scalar.copy(y[2][:], acc_two[:])
         acc_last = first_product(LAST_TILE, all_cells, "y_acc3", 6)
-        first_product(LAST_TILE, all_cells, "warm_up1", 5)
         for m in range(HALVES):
             interleave(nc.scalar.copy, w2_grouped[:, span(PACK * m, PACK * (m + 1))], w2_raw[m][:])
         y.append(sb([P, S], F32, "y3", tag="w2_raw1"))

@@ -89,9 +89,10 @@ def tile_picked_ynca_tanh_p_kernel(
         for r in range(SCALE_ROWS):
             nc.sync.dma_start(scale_table[r:P:QUADRANT, :].bitcast(I32), x_scales[0, r::SCALE_ROWS, :].bitcast(I32))
         nc.sync.dma_start(word_table[:, AHEAD:].bitcast(I32), word_rows[:, AHEAD:])
+        nc.sync.dma_start(pos_sb[1][:], pos2)
         nc.sync.dma_start(w1_middle[:], w1_rows[:, :, span(1, LAST_TILE)])
-        for n, pos in enumerate((pos1, pos2)):
-            nc.sync.dma_start(pos_sb[n][:], pos)
+        nc.sync.dma_start(pos_sb[0][:], pos1)
+        for n in range(NEIGHBOURS):
             nc.sync.dma_start(kern_sb[n][:], kern[n])
         nc.sync.dma_start(w1_last[:], w1_rows[:, :, span(LAST_TILE)])
         for m in range(HALVES):
@@ -236,8 +237,9 @@ def tile_picked_ynca_tanh_p_kernel(
             return lambda n: sb([P, P], F32, "seen%d_%d_%d" % (LAST_TILE, n, b))[:]
 
         quantise_w1(range(1, LAST_TILE), nc.vector.tensor_copy)
-        for i, cols in enumerate(cell_halves):
-            nc.scalar.copy(y[1][:, cols], first_product(1, cols, "y_acc1_%d" % i, 4 + i)[:])
+        fetched = sb([P, S], F32, "fetched")
+        nc.scalar.activation(fetched[:], y[0][:].indirect(pos_sb[1][:]), ACT.Copy)
+        nc.scalar.copy(y[1][:], first_product(1, all_cells, "y_acc1", 2)[:])
         y.append(placed.tile([P, S], F32, name="y2", align_bytes=64, offset=raw_at + ROW_BYTES // 2))
         acc_two = first_product(2, all_cells, "y_acc2", 0)
 
@@ -246,15 +248,19 @@ def tile_picked_ynca_tanh_p_kernel(
         def early_sum(t, b):
             return low[b // 2][:, b % 2, span(t)]
 
-        for t in range(EARLY):
-            for b in range(BLOCKS - t):
-                own(early_sum(t, b), t, b, t == 0 and b % 2 == 0)
+        for b in range(BLOCKS):
+            own(early_sum(0, b), 0, b, b % 2 == 0)
         for n in range(NEIGHBOURS):
             seen = sb([P, S], F32, "seen0_%d" % n, tag=None if n else "w1_middle")
-            look_up(0, n, all_cells, seen[:])
+            if n:
+                nc.vector.tensor_tensor(seen[:], fetched[:], kern_sb[n][:], ALU.mult)
+            else:
+                look_up(0, n, all_cells, seen[:])
             for b in range(BLOCKS):
                 add_turned(early_sum(0, b), seen[:, span(b)])
 
+        seen_ahead = sb([P, LAST_BLOCK * P], F32, "seen1_0")
+        look_up(1, 0, span(0, LAST_BLOCK), seen_ahead[:])
         quantise_w1(range(LAST_TILE, TILES), nc.scalar.copy)
         nc.scalar.copy(y[2][:], acc_two[:])
         acc_last = first_product(LAST_TILE, all_cells, "y_acc3", 6)
@@ -264,17 +270,15 @@ def tile_picked_ynca_tanh_p_kernel(
         nc.scalar.copy(y[LAST_TILE][:], acc_last[:])
 
         pieces = LAST_BLOCK + 2
-        seen_middle = placed.tile(
-            [P, NEIGHBOURS, pieces * P],
-            F32,
-            name="seen1",
-            align_bytes=64,
-            offset=raw_at + ROW_BYTES // 4 - NEIGHBOURS * pieces * P * 4,
-        )
+        seen_middle = sb([P, NEIGHBOURS, pieces * P], F32, "seen1", tag="w1_grouped%d" % LAST_TILE)
+        for b in range(LAST_BLOCK):
+            own(early_sum(1, b), 1, b, False)
         for n in range(NEIGHBOURS):
-            look_up(1, n, span(0, LAST_BLOCK), seen_middle[:, n, span(0, LAST_BLOCK)])
+            seen = seen_middle[:, n, span(0, LAST_BLOCK)] if n else seen_ahead[:]
+            if n:
+                look_up(1, n, span(0, LAST_BLOCK), seen)
             for b in range(LAST_BLOCK):
-                add_turned(early_sum(1, b), seen_middle[:, n, span(b)], stop=(n == NEIGHBOURS - 1 and b > 0))
+                add_turned(early_sum(1, b), seen[:, span(b)], stop=(n == NEIGHBOURS - 1 and b > 0))
 
         fire_turned = bank([P, P], "fire_turned", 6)
         nc.tensor.transpose(fire_turned[:], fire_rows[:], ident[:])

@@ -79,7 +79,8 @@ def tile_picked_ynca_tanh_p_kernel(
         kern_sb = [sb([P, S], F32, "kern%d" % n) for n in range(NEIGHBOURS)]
         pos_sb = [keep.tile([P, S // PER_COL], U16, name="pos%d" % n) for n in range(NEIGHBOURS)]
         w2_raw = [sb([P, PACK, P], F32, "w2_raw%d" % m) for m in range(HALVES)]
-        fire_rows = sb([P, P], F32, "fire_rows")
+        fire_at = 8 * ROW_BYTES
+        fire_rows = placed.tile([P, P], F32, name="fire_rows", align_bytes=64, offset=fire_at)
         cur_sb = sb([P, HALVES, S], F32, "cur_sb")
 
         nc.sync.dma_start(w1_first[:], w1_rows[:, :, span(0)])
@@ -180,22 +181,11 @@ def tile_picked_ynca_tanh_p_kernel(
                 )
             return grouped
 
-        def quantise_w2(m):
-            nc.vector.quantize_mx(
-                out=w2_codes[:, span(m)].bitcast(FP8X4),
-                scales=w2_scale[:, span(m)],
-                in_=w2_grouped[:, span(PACK * m, PACK * (m + 1))],
-            )
-
         def second_product(first, last, grouped, numbers, with_weights=False):
             width = (last - first) * P
-            h_codes = sb([P, width], U32, "h_codes%d" % first)
+            h_codes = sb([P, width], U32, "h_codes%d" % first, tag="w2_raw1" if with_weights else None)
             h_scale = sb([P, width], U8, "h_scale%d" % first)
-            if with_weights:
-                quantise_w2(0)
             nc.vector.quantize_mx(out=h_codes[:].bitcast(FP8X4), scales=h_scale[:], in_=grouped[:])
-            if with_weights:
-                quantise_w2(1)
             per = HALVES // len(numbers)
             rr = [bank([P, per, width], "rr%d_%d" % (first, i), number) for i, number in enumerate(numbers)]
             for m in range(HALVES):
@@ -305,7 +295,8 @@ def tile_picked_ynca_tanh_p_kernel(
         second = [bank([P, P], "pre_second%d" % t, number) for t, number in ((2, 7), (LAST_TILE, 2))]
         for i, acc in enumerate(second):
             own(acc[:], EARLY + i, 2, True)
-        held = sb([P, 3 * NEIGHBOURS, P], F32, "seen_held", tag="fire_rows")
+        held = placed.tile([P, 3 * NEIGHBOURS, P], F32, name="seen_held", align_bytes=64, offset=fire_at + 256)
+        w2_codes = placed.tile([P, N], U32, name="w2_codes", align_bytes=64, offset=fire_at + 256 - 4 * N)
 
         def held_piece(i):
             return lambda n: held[:, NEIGHBOURS * i + n, :]
@@ -314,6 +305,7 @@ def tile_picked_ynca_tanh_p_kernel(
         rectify(2, range(2, LAST_TILE), second[0][:])
         neighbours(second[1][:], LAST_TILE, 2, fresh(2), True)
         rectify(2, range(LAST_TILE, TILES), second[1][:])
+        nc.vector.quantize_mx(out=w2_codes[:].bitcast(FP8X4), scales=w2_scale[:], in_=w2_grouped[:])
         grouped_second = turn_back(*GROUPS[1], (4,))
 
         middle = bank([P, 2 * P], "pre_middle", 6)
@@ -325,7 +317,6 @@ def tile_picked_ynca_tanh_p_kernel(
             neighbours(middle[:, span(t - 1)], t, LAST_BLOCK, held_piece(t), t == LAST_TILE - 1)
         rectify(LAST_BLOCK, range(1, LAST_TILE), middle[:])
         neighbours(final[:], LAST_TILE, LAST_BLOCK, fresh(LAST_BLOCK), True)
-        w2_codes = sb([P, N], U32, "w2_codes", tag="w2_raw1")
         rr_first = second_product(*GROUPS[0], grouped_first, (5, 0), with_weights=True)
         rectify(LAST_BLOCK, range(LAST_TILE, TILES), final[:])
         grouped_last = turn_back(*GROUPS[2], (1,))

@@ -80,7 +80,7 @@ def tile_picked_ynca_tanh_p_kernel(
         pos_sb = [keep.tile([P, S // PER_COL], U16, name="pos%d" % n) for n in range(NEIGHBOURS)]
         w2_raw = [sb([P, PACK, P], F32, "w2_raw%d" % m) for m in range(HALVES)]
         fire_at = 8 * ROW_BYTES
-        fire_rows = placed.tile([P, P], F32, name="fire_rows", align_bytes=64, offset=fire_at)
+        fire_rows = sb([P, P], F32, "fire_rows")
         cur_sb = sb([P, HALVES, S], F32, "cur_sb")
 
         nc.sync.dma_start(w1_first[:], w1_rows[:, :, span(0)])
@@ -96,9 +96,9 @@ def tile_picked_ynca_tanh_p_kernel(
         for n in range(NEIGHBOURS):
             nc.sync.dma_start(kern_sb[n][:], kern[n])
         nc.sync.dma_start(w1_last[:], w1_rows[:, :, span(LAST_TILE)])
+        nc.sync.dma_start(fire_rows[:], fire[0 : P // BLOCKS, :].rearrange("r (b j) -> (r b) j", j=P))
         for m in range(HALVES):
             nc.sync.dma_start(w2_raw[m][:], w2.rearrange("(p t) c -> p t c", t=PACK)[:, :, span(m)])
-        nc.sync.dma_start(fire_rows[:], fire[0 : P // BLOCKS, :].rearrange("r (b j) -> (r b) j", j=P))
         nc.sync.dma_start(cur_sb[:], cur.rearrange("(h p) j -> p h j", p=P))
 
         ident = sb([P, P], F32, "ident")
@@ -158,13 +158,13 @@ def tile_picked_ynca_tanh_p_kernel(
         def add_turned(target, term, start=False, stop=False):
             nc.tensor.matmul(target, term, ident[:], start=start, stop=stop, is_transpose=True)
 
-        def rectify(b, tiles, pre):
+        def rectify(b, tiles, pre, fire_of=None):
             rows = h_rows[b][:].rearrange("j (u p e) -> j u p e", u=2, e=2)
             nc.scalar.activation(
                 rows[:, :, tiles.start * (P // PACK) : tiles.stop * (P // PACK), :],
                 pre.rearrange("j (p u e) -> j u p e", u=2, e=2),
                 ACT.Relu,
-                scale=fire_col[:, b : b + 1],
+                scale=(fire_col if fire_of is None else fire_of)[:, b : b + 1],
             )
 
         def turn_back(first, last, numbers):
@@ -181,11 +181,22 @@ def tile_picked_ynca_tanh_p_kernel(
                 )
             return grouped
 
+        def quantise_w2(m):
+            nc.vector.quantize_mx(
+                out=w2_codes[:, span(m)].bitcast(FP8X4),
+                scales=w2_scale[:, span(m)],
+                in_=w2_grouped[:, span(PACK * m, PACK * (m + 1))],
+            )
+
         def second_product(first, last, grouped, numbers, with_weights=False):
             width = (last - first) * P
-            h_codes = sb([P, width], U32, "h_codes%d" % first, tag="w2_raw1" if with_weights else None)
+            h_codes = sb([P, width], U32, "h_codes%d" % first)
             h_scale = sb([P, width], U8, "h_scale%d" % first)
+            if with_weights:
+                quantise_w2(0)
             nc.vector.quantize_mx(out=h_codes[:].bitcast(FP8X4), scales=h_scale[:], in_=grouped[:])
+            if with_weights:
+                quantise_w2(1)
             per = HALVES // len(numbers)
             rr = [bank([P, per, width], "rr%d_%d" % (first, i), number) for i, number in enumerate(numbers)]
             for m in range(HALVES):
@@ -253,11 +264,26 @@ def tile_picked_ynca_tanh_p_kernel(
         look_up(1, 0, span(0, LAST_BLOCK), seen_ahead[:])
         quantise_w1(range(LAST_TILE, TILES), nc.scalar.copy)
         nc.scalar.copy(y[2][:], acc_two[:])
-        acc_last = first_product(LAST_TILE, all_cells, "y_acc3", 6)
+        acc_last = first_product(LAST_TILE, cell_halves[0], "y_acc3", 6)
+        beside = bank([P, 3 * P], "y_acc3_fire", 5)
+        nc.tensor.transpose(beside[:, span(2)], fire_rows[:], ident[:])
+        nc.tensor.matmul_mx(
+            out=beside[:, span(0, 2)],
+            lhsT=w1_codes[LAST_TILE].bitcast(FP8X4),
+            lhsT_scale=w1_scale[LAST_TILE],
+            rhs=x_codes[:, cell_halves[1]].bitcast(FP8X4),
+            rhs_scale=x_scale[:, cell_halves[1]],
+            start=True,
+            stop=True,
+        )
         for m in range(HALVES):
             interleave(nc.scalar.copy, w2_grouped[:, span(PACK * m, PACK * (m + 1))], w2_raw[m][:])
         y.append(sb([P, S], F32, "y3", tag="w2_raw1"))
-        nc.scalar.copy(y[LAST_TILE][:], acc_last[:])
+        nc.scalar.copy(y[LAST_TILE][:, cell_halves[0]], acc_last[:])
+        nc.scalar.copy(y[LAST_TILE][:, cell_halves[1]], beside[:, span(0, 2)])
+        fire_first = placed.tile([P, 2], F32, name="fire_first", align_bytes=64, offset=fire_at)
+        nc.scalar.copy(fire_first[:], beside[:, 2 * P : 2 * P + 2])
+        nc.scalar.copy(fire_col[:], beside[:, 2 * P : 2 * P + BLOCKS])
 
         pieces = LAST_BLOCK + 2
         seen_middle = sb([P, NEIGHBOURS, pieces * P], F32, "seen1", tag="w1_grouped%d" % LAST_TILE)
@@ -270,12 +296,9 @@ def tile_picked_ynca_tanh_p_kernel(
             for b in range(LAST_BLOCK):
                 add_turned(early_sum(1, b), seen[:, span(b)], stop=(n == NEIGHBOURS - 1 and b > 0))
 
-        fire_turned = bank([P, P], "fire_turned", 6)
-        nc.tensor.transpose(fire_turned[:], fire_rows[:], ident[:])
-        nc.scalar.copy(fire_col[:], fire_turned[:, 0:BLOCKS])
         for b in range(BLOCKS):
             tiles = 1 if b == LAST_BLOCK else EARLY
-            rectify(b, range(tiles), low[b // 2][:, b % 2, span(0, tiles)])
+            rectify(b, range(tiles), low[b // 2][:, b % 2, span(0, tiles)], fire_first if b < 2 else None)
 
         high = [bank([P, 2 * P], "pre_high%d" % b, 1 + b) for b in range(2)]
         for t in range(EARLY, TILES):
@@ -295,17 +318,15 @@ def tile_picked_ynca_tanh_p_kernel(
         second = [bank([P, P], "pre_second%d" % t, number) for t, number in ((2, 7), (LAST_TILE, 2))]
         for i, acc in enumerate(second):
             own(acc[:], EARLY + i, 2, True)
-        held = placed.tile([P, 3 * NEIGHBOURS, P], F32, name="seen_held", align_bytes=64, offset=fire_at + 256)
-        w2_codes = placed.tile([P, N], U32, name="w2_codes", align_bytes=64, offset=fire_at + 256 - 4 * N)
+        held = placed.tile([P, 5 * NEIGHBOURS, P], F32, name="seen_held", align_bytes=64, offset=fire_at)
 
         def held_piece(i):
             return lambda n: held[:, NEIGHBOURS * i + n, :]
 
         neighbours(second[0][:], 2, 2, held_piece(0), True)
         rectify(2, range(2, LAST_TILE), second[0][:])
-        neighbours(second[1][:], LAST_TILE, 2, fresh(2), True)
+        neighbours(second[1][:], LAST_TILE, 2, held_piece(3), True)
         rectify(2, range(LAST_TILE, TILES), second[1][:])
-        nc.vector.quantize_mx(out=w2_codes[:].bitcast(FP8X4), scales=w2_scale[:], in_=w2_grouped[:])
         grouped_second = turn_back(*GROUPS[1], (4,))
 
         middle = bank([P, 2 * P], "pre_middle", 6)
@@ -316,7 +337,8 @@ def tile_picked_ynca_tanh_p_kernel(
         for t in range(1, LAST_TILE):
             neighbours(middle[:, span(t - 1)], t, LAST_BLOCK, held_piece(t), t == LAST_TILE - 1)
         rectify(LAST_BLOCK, range(1, LAST_TILE), middle[:])
-        neighbours(final[:], LAST_TILE, LAST_BLOCK, fresh(LAST_BLOCK), True)
+        neighbours(final[:], LAST_TILE, LAST_BLOCK, held_piece(4), True)
+        w2_codes = sb([P, N], U32, "w2_codes", tag="w2_raw1")
         rr_first = second_product(*GROUPS[0], grouped_first, (5, 0), with_weights=True)
         rectify(LAST_BLOCK, range(LAST_TILE, TILES), final[:])
         grouped_last = turn_back(*GROUPS[2], (1,))

from contextlib import ExitStack

import concourse.mybir as mybir
from concourse.masks import make_identity

K, T, S, H, N = 512, 2048, 512, 512, 256
FLOPS = 2 * K * H * S + 2 * H * N * S

F32 = mybir.dt.float32
BF16 = mybir.dt.bfloat16
I32 = mybir.dt.int32
U32 = mybir.dt.uint32
U16 = mybir.dt.uint16
U8 = mybir.dt.uint8
FP8X4 = mybir.dt.float8_e4m3fn_x4
ALU = mybir.AluOpType
ACT = mybir.ActivationFunctionType

P = 128
PACK = 4
PER_COL = 16
QUADRANT = 32
NEIGHBOURS = 2
TILES = H // P
BLOCKS = S // P
HALVES = N // P
SCALE_ROWS = 4
LAST_TILE = TILES - 1
LAST_BLOCK = BLOCKS - 1
EARLY = 2
SPARE = 16
AHEAD = T // 4
ROW_BYTES = 4 * S
GROUPS = ((0, 2), (2, 3), (3, 4))


def span(first, last=None):
    return slice(first * P, (first + 1 if last is None else last) * P)


def entries(offsets, cols):
    return offsets[:, cols.start // PER_COL : cols.stop // PER_COL]


def interleave(copy, grouped, raw):
    copy(
        out=grouped.rearrange("p (c i t) -> p c t i", i=4, t=PACK),
        in_=raw.rearrange("p t (c i) -> p c t i", i=4),
    )


def tile_picked_ynca_tanh_p_kernel(
    tc, x_words, x_scales, w1, w2, kern, cur, fire, offs, pos1, pos2, out
):
    nc = tc.nc
    with ExitStack() as ctx:
        keep = ctx.enter_context(tc.tile_pool(name="keep", bufs=1))
        banks = ctx.enter_context(tc.psum_pool(name="banks", bufs=1))
        placed = ctx.enter_context(tc.tile_pool(name="placed", bufs=1))
        raw_at = 4 * ROW_BYTES

        def sb(shape, dtype, name, tag=None):
            return keep.tile(shape, dtype, name=name, tag=tag or name, align_bytes=64)

        def bank(shape, name, number):
            return banks.tile(shape, F32, name=name, tag="bank%d" % number)

        scale_table = sb([P, T], U8, "scale_table")
        nc.vector.memset(scale_table[:].bitcast(I32), 0)

        offs_sb = keep.tile([P, S // PER_COL], U16, name="offs_sb")

        w1_rows = w1.rearrange("(p t) c -> p t c", t=PACK)
        w1_first = sb([P, PACK, P], F32, "w1_first")
        w1_middle = sb([P, PACK, 2 * P], F32, "w1_middle")
        w1_last = placed.tile([P, PACK, P], F32, name="w1_last", align_bytes=64, offset=raw_at)
        w1_raw = [w1_first[:], w1_middle[:, :, span(0)], w1_middle[:, :, span(1)], w1_last[:]]
        word_table = sb([P, T], U32, "word_table")
        kern_sb = [sb([P, S], F32, "kern%d" % n) for n in range(NEIGHBOURS)]
        pos_sb = [keep.tile([P, S // PER_COL], U16, name="pos%d" % n) for n in range(NEIGHBOURS)]
        w2_raw = [sb([P, PACK, P], F32, "w2_raw%d" % m) for m in range(HALVES)]
        fire_at = 8 * ROW_BYTES
        fire_rows = sb([P, P], F32, "fire_rows")
        cur_sb = sb([P, HALVES, S], F32, "cur_sb")

        nc.sync.dma_start(w1_first[:], w1_rows[:, :, span(0)])
        nc.sync.dma_start(offs_sb[:], offs)
        word_rows = x_words[0].rearrange("p n t -> p (n t)").bitcast(I32)
        nc.sync.dma_start(word_table[:, :AHEAD].bitcast(I32), word_rows[:, :AHEAD])
        for r in range(SCALE_ROWS):
            nc.sync.dma_start(scale_table[r:P:QUADRANT, :].bitcast(I32), x_scales[0, r::SCALE_ROWS, :].bitcast(I32))
        nc.sync.dma_start(word_table[:, AHEAD:].bitcast(I32), word_rows[:, AHEAD:])
        nc.sync.dma_start(pos_sb[1][:], pos2)
        nc.sync.dma_start(w1_middle[:], w1_rows[:, :, span(1, LAST_TILE)])
        nc.sync.dma_start(pos_sb[0][:], pos1)
        for n in range(NEIGHBOURS):
            nc.sync.dma_start(kern_sb[n][:], kern[n])
        nc.sync.dma_start(w1_last[:], w1_rows[:, :, span(LAST_TILE)])
        nc.sync.dma_start(fire_rows[:], fire[0 : P // BLOCKS, :].rearrange("r (b j) -> (r b) j", j=P))
        for m in range(HALVES):
            nc.sync.dma_start(w2_raw[m][:], w2.rearrange("(p t) c -> p t c", t=PACK)[:, :, span(m)])
        nc.sync.dma_start(cur_sb[:], cur.rearrange("(h p) j -> p h j", p=P))

        ident = sb([P, P], F32, "ident")
        make_identity(nc, ident[:])

        x_scale = sb([P, S], U8, "x_scale")
        nc.vector.tensor_copy(x_scale[:], scale_table[:].indirect(offs_sb[:]))

        w1_codes = []
        w1_scale = []

        def quantise_w1(tiles, copy):
            grouped = [sb([P, P * PACK], BF16, "w1_grouped%d" % t) for t in tiles]
            for i, t in enumerate(tiles):
                interleave(copy, grouped[i][:], w1_raw[t])
            for i, t in enumerate(tiles):
                codes = sb([P, P], U32, "w1_codes%d" % t)
                scale = sb([P, P], U8, "w1_scale%d" % t)
                w1_codes.append(codes[:])
                w1_scale.append(scale[:])
                nc.vector.quantize_mx(out=codes[:].bitcast(FP8X4), scales=scale[:], in_=grouped[i][:])

        x_codes = sb([P, S], U32, "x_codes")
        y = [sb([P, S + SPARE if t == 0 else S], F32, "y%d" % t) for t in range(EARLY)]
        nc.gpsimd.memset(y[0][:, S:], 0.0)

        def first_product(t, cols, name, number):
            acc = bank([P, cols.stop - cols.start], name, number)
            nc.tensor.matmul_mx(
                out=acc[:],
                lhsT=w1_codes[t].bitcast(FP8X4),
                lhsT_scale=w1_scale[t],
                rhs=x_codes[:, cols].bitcast(FP8X4),
                rhs_scale=x_scale[:, cols],
                start=True,
                stop=True,
            )
            return acc

        quantise_w1(range(0, 1), nc.scalar.copy)
        cell_halves = (span(0, BLOCKS // 2), span(BLOCKS // 2, BLOCKS))
        for cols in cell_halves:
            nc.vector.tensor_copy(x_codes[:, cols], word_table[:].indirect(entries(offs_sb, cols)))
        for i, cols in enumerate([cell_halves[0]] + [span(b) for b in range(BLOCKS // 2, BLOCKS)]):
            acc = first_product(0, cols, "y_acc0_%d" % cols.start, i)
            nc.scalar.copy(y[0][:, cols], acc[:])

        fire_col = sb([P, BLOCKS], F32, "fire_col")
        w2_scale = sb([P, N], U8, "w2_scale")
        w2_grouped = sb([P, N * PACK], BF16, "w2_grouped")
        h_rows = [sb([P, H], BF16, "h_rows%d" % b) for b in range(BLOCKS)]
        all_cells = span(0, BLOCKS)

        def look_up(t, n, cols, seen):
            nc.vector.tensor_tensor(seen, y[t][:].indirect(entries(pos_sb[n], cols)), kern_sb[n][:, cols], ALU.mult)

        def add_turned(target, term, start=False, stop=False):
            nc.tensor.matmul(target, term, ident[:], start=start, stop=stop, is_transpose=True)

        def rectify(b, tiles, pre, fire_of=None):
            rows = h_rows[b][:].rearrange("j (u p e) -> j u p e", u=2, e=2)
            nc.scalar.activation(
                rows[:, :, tiles.start * (P // PACK) : tiles.stop * (P // PACK), :],
                pre.rearrange("j (p u e) -> j u p e", u=2, e=2),
                ACT.Relu,
                scale=(fire_col if fire_of is None else fire_of)[:, b : b + 1],
            )

        def turn_back(first, last, numbers):
            grouped = sb([P, (last - first) * P * PACK], BF16, "h_grouped%d" % first)
            words = grouped[:].bitcast(F32)
            for b in range(first, last):
                turned = bank([P, 2, P], "h_turned%d" % b, numbers[b - first])
                pairs = h_rows[b][:].bitcast(F32)
                for u in range(2):
                    nc.tensor.transpose(turned[:, u, :], pairs[:, span(u)], ident[:])
                nc.scalar.copy(
                    words[:, span(2 * (b - first), 2 * (b - first + 1))].rearrange("p (j u) -> p j u", u=2),
                    turned[:].rearrange("p u j -> p j u"),
                )
            return grouped

        def quantise_w2(m):
            nc.vector.quantize_mx(
                out=w2_codes[:, span(m)].bitcast(FP8X4),
                scales=w2_scale[:, span(m)],
                in_=w2_grouped[:, span(PACK * m, PACK * (m + 1))],
            )

        def second_product(first, last, grouped, numbers, with_weights=False):
            width = (last - first) * P
            h_codes = sb([P, width], U32, "h_codes%d" % first)
            h_scale = sb([P, width], U8, "h_scale%d" % first)
            if with_weights:
                quantise_w2(0)
            nc.vector.quantize_mx(out=h_codes[:].bitcast(FP8X4), scales=h_scale[:], in_=grouped[:])
            if with_weights:
                quantise_w2(1)
            per = HALVES // len(numbers)
            rr = [bank([P, per, width], "rr%d_%d" % (first, i), number) for i, number in enumerate(numbers)]
            for m in range(HALVES):
                nc.tensor.matmul_mx(
                    out=rr[m // per][:, m % per, :],
                    lhsT=w2_codes[:, span(m)].bitcast(FP8X4),
                    lhsT_scale=w2_scale[:, span(m)],
                    rhs=h_codes[:].bitcast(FP8X4),
                    rhs_scale=h_scale[:],
                    start=True,
                    stop=True,
                )
            return rr

        out_rows = out.rearrange("(m p) j -> p m j", p=P)

        def update(first, last, rr, i, moved_tag=None, state=None):
            cols = span(first, last)
            per = HALVES // len(rr)
            rows = slice(i * per, (i + 1) * per)
            shape = [P, per, cols.stop - cols.start]
            moved = sb(shape, F32, "moved%d_%d" % (first, i), tag=moved_tag)
            nc.vector.tensor_tensor(moved[:], rr[i][:], cur_sb[:, rows, cols], ALU.add)
            if state is None:
                state = sb(shape, F32, "state%d_%d" % (first, i))[:]
            nc.scalar.activation(state, moved[:], ACT.Tanh)
            nc.sync.dma_start(out_rows[:, rows, cols], state)

        def own(target, t, b, start):
            add_turned(target, y[t][:, span(b)], start=start)

        def neighbours(target, t, b, seen, stop):
            for n in range(NEIGHBOURS):
                term = seen(n)
                look_up(t, n, span(b), term)
                add_turned(target, term, stop=(stop and n == NEIGHBOURS - 1))

        def fresh(b):
            return lambda n: sb([P, P], F32, "seen%d_%d_%d" % (LAST_TILE, n, b))[:]

        quantise_w1(range(1, LAST_TILE), nc.vector.tensor_copy)
        fetched = sb([P, S], F32, "fetched")
        nc.scalar.activation(fetched[:], y[0][:].indirect(pos_sb[1][:]), ACT.Copy)
        nc.scalar.copy(y[1][:], first_product(1, all_cells, "y_acc1", 2)[:])
        y.append(placed.tile([P, S], F32, name="y2", align_bytes=64, offset=raw_at + ROW_BYTES // 2))
        acc_two = first_product(2, all_cells, "y_acc2", 0)

        low = [bank([P, 2, EARLY * P], "pre_low%d" % i, 3 + i) for i in range(BLOCKS // 2)]

        def early_sum(t, b):
            return low[b // 2][:, b % 2, span(t)]

        for b in range(BLOCKS):
            own(early_sum(0, b), 0, b, b % 2 == 0)
        for n in range(NEIGHBOURS):
            seen = sb([P, S], F32, "seen0_%d" % n, tag=None if n else "w1_middle")
            if n:
                nc.vector.tensor_tensor(seen[:], fetched[:], kern_sb[n][:], ALU.mult)
            else:
                look_up(0, n, all_cells, seen[:])
            for b in range(BLOCKS):
                add_turned(early_sum(0, b), seen[:, span(b)])

        seen_ahead = sb([P, LAST_BLOCK * P], F32, "seen1_0")
        look_up(1, 0, span(0, LAST_BLOCK), seen_ahead[:])
        quantise_w1(range(LAST_TILE, TILES), nc.scalar.copy)
        nc.scalar.copy(y[2][:], acc_two[:])
        acc_last = first_product(LAST_TILE, cell_halves[0], "y_acc3", 6)
        beside = bank([P, 3 * P], "y_acc3_fire", 5)
        nc.tensor.transpose(beside[:, span(2)], fire_rows[:], ident[:])
        nc.tensor.matmul_mx(
            out=beside[:, span(0, 2)],
            lhsT=w1_codes[LAST_TILE].bitcast(FP8X4),
            lhsT_scale=w1_scale[LAST_TILE],
            rhs=x_codes[:, cell_halves[1]].bitcast(FP8X4),
            rhs_scale=x_scale[:, cell_halves[1]],
            start=True,
            stop=True,
        )
        for m in range(HALVES):
            interleave(nc.scalar.copy, w2_grouped[:, span(PACK * m, PACK * (m + 1))], w2_raw[m][:])
        y.append(sb([P, S], F32, "y3", tag="w2_raw1"))
        nc.scalar.copy(y[LAST_TILE][:, cell_halves[0]], acc_last[:])
        nc.scalar.copy(y[LAST_TILE][:, cell_halves[1]], beside[:, span(0, 2)])
        fire_first = placed.tile([P, 2], F32, name="fire_first", align_bytes=64, offset=fire_at)
        nc.scalar.copy(fire_first[:], beside[:, 2 * P : 2 * P + 2])
        nc.scalar.copy(fire_col[:], beside[:, 2 * P : 2 * P + BLOCKS])

        pieces = LAST_BLOCK + 2
        seen_middle = sb([P, NEIGHBOURS, pieces * P], F32, "seen1", tag="w1_grouped%d" % LAST_TILE)
        for b in range(LAST_BLOCK):
            own(early_sum(1, b), 1, b, False)
        for n in range(NEIGHBOURS):
            seen = seen_middle[:, n, span(0, LAST_BLOCK)] if n else seen_ahead[:]
            if n:
                look_up(1, n, span(0, LAST_BLOCK), seen)
            for b in range(LAST_BLOCK):
                add_turned(early_sum(1, b), seen[:, span(b)], stop=(n == NEIGHBOURS - 1 and b > 0))

        for b in range(BLOCKS):
            tiles = 1 if b == LAST_BLOCK else EARLY
            rectify(b, range(tiles), low[b // 2][:, b % 2, span(0, tiles)], fire_first if b < 2 else None)

        high = [bank([P, 2 * P], "pre_high%d" % b, 1 + b) for b in range(2)]
        for t in range(EARLY, TILES):
            for b in range(2):
                own(high[b][:, span(t - EARLY)], t, b, t == EARLY)
        for n in range(NEIGHBOURS):
            seen = seen_middle[:, n, span(LAST_BLOCK, pieces)]
            look_up(2, n, span(0, 2), seen)
            for b in range(2):
                add_turned(high[b][:, span(0)], seen[:, span(b)])
        for b in range(2):
            neighbours(high[b][:, span(1)], LAST_TILE, b, fresh(b), True)
        for b in range(2):
            rectify(b, range(EARLY, TILES), high[b][:])
        grouped_first = turn_back(*GROUPS[0], (6, 3))

        second = [bank([P, P], "pre_second%d" % t, number) for t, number in ((2, 7), (LAST_TILE, 2))]
        for i, acc in enumerate(second):
            own(acc[:], EARLY + i, 2, True)
        held = placed.tile([P, 5 * NEIGHBOURS, P], F32, name="seen_held", align_bytes=64, offset=fire_at)

        def held_piece(i):
            return lambda n: held[:, NEIGHBOURS * i + n, :]

        neighbours(second[0][:], 2, 2, held_piece(0), True)
        rectify(2, range(2, LAST_TILE), second[0][:])
        neighbours(second[1][:], LAST_TILE, 2, held_piece(3), True)
        rectify(2, range(LAST_TILE, TILES), second[1][:])
        grouped_second = turn_back(*GROUPS[1], (4,))

        middle = bank([P, 2 * P], "pre_middle", 6)
        final = bank([P, P], "pre_final", 2)
        for t in range(1, LAST_TILE):
            own(middle[:, span(t - 1)], t, LAST_BLOCK, t == 1)
        own(final[:], LAST_TILE, LAST_BLOCK, True)
        for t in range(1, LAST_TILE):
            neighbours(middle[:, span(t - 1)], t, LAST_BLOCK, held_piece(t), t == LAST_TILE - 1)
        rectify(LAST_BLOCK, range(1, LAST_TILE), middle[:])
        neighbours(final[:], LAST_TILE, LAST_BLOCK, held_piece(4), True)
        w2_codes = sb([P, N], U32, "w2_codes", tag="w2_raw1")
        rr_first = second_product(*GROUPS[0], grouped_first, (5, 0), with_weights=True)
        rectify(LAST_BLOCK, range(LAST_TILE, TILES), final[:])
        grouped_last = turn_back(*GROUPS[2], (1,))

        state_first = sb([P, HALVES, 2 * P], F32, "state_first", tag="h_rows%d" % LAST_BLOCK)
        update(*GROUPS[0], rr_first, 0, state=state_first[:, 0:1, :])
        rr_second = second_product(*GROUPS[1], grouped_second, (2,))
        update(*GROUPS[0], rr_first, 1, moved_tag="h_grouped%d" % GROUPS[1][0], state=state_first[:, 1:2, :])
        rr_last = second_product(*GROUPS[2], grouped_last, (7, 3))
        update(*GROUPS[1], rr_second, 0, moved_tag="h_grouped%d" % GROUPS[2][0])
        for i in range(HALVES):
            update(*GROUPS[2], rr_last, i)
